import numpy as np, ml_dtypes
CORES = [3,11,19,27,35,43,51,59]
N = 8
BF = ml_dtypes.bfloat16
def gentries(a):
    return np.ascontiguousarray(a.reshape(8, 16, -1).transpose(0, 2, 1)).reshape(8, -1)
def gtable(e):
    e = np.asarray(e); return np.ascontiguousarray(e.reshape(8, -1, 16).transpose(0, 2, 1)).reshape(128, -1).astype(np.int32)
NV, S, TOP, G = 1536, 384, 192, 32
K, K2, LIM, ST, RO = 192, 192, 704, 432, 3
M = NV - S - TOP; W = NV + (N - 1) * G
FANS = np.array([1, 2, 2, 2, 3, 3, 4, 6, 16])
def twin(d):
    g = np.arange(8)
    return (7 - g, (8 - g) % 8, g)[(d - 1) % 3]
def wire(rng, cut):
    p = np.zeros((16, NV), np.int64)
    for c, im, f in cut:
        b = np.stack([rng.permutation(im) for _ in range(f)])
        p[:, c] = b[rng.permutation(np.concatenate([np.arange(f), rng.integers(0, f, 16 - f)]))]
    return p
def layered(rng, fans):
    pool = np.argsort(np.concatenate([np.arange(NV), rng.integers(0, NV, W - NV)]) + rng.random(W))
    lag = int(rng.choice(np.array([0, 32, 64, 128]))); cut = []
    for a in range(0, NV - S, 128):
        o = S + a + rng.permutation(128); im = rng.permutation(pool[lag + a:lag + a + 128])
        for i in range(0, 128, 32): cut.append((o[i:i + 32], im[i:i + 32], int(rng.choice(fans))))
    rest = rng.permutation(np.concatenate([pool[:lag], pool[lag + NV - S:]])); o = rng.permutation(S)
    for i in range(0, S, 64): cut.append((o[i:i + 64], rest[i:i + 64], int(rng.choice(fans))))
    return wire(rng, cut)
def flat(rng, pool):
    p = np.zeros((16, NV), np.int64)
    for k in range(16):
        o = rng.permutation(pool)[:TOP]; p[k, NV - TOP:] = o
        p[k, :NV - TOP] = rng.permutation(np.setdiff1d(np.arange(W), o))[:NV - TOP]
    return p
def aim(p, k, v, u):
    w = np.nonzero(p[k] == u)[0]
    if len(w): p[k, w[0]] = p[k, v]
    p[k, v] = u
def sweep(rng, miss):
    o = rng.permutation(NV); p = np.zeros((16, NV), np.int64); x = S + int(rng.integers(0, M))
    for k in range(16):
        a = o[k::16]; v = NV - TOP + rng.permutation(TOP - 3)[:len(a)]
        p[k, v] = a; p[k, np.setdiff1d(np.arange(NV), v)] = rng.permutation(np.setdiff1d(np.arange(W), a))[:NV - len(a)]
        if miss: aim(p, k, S, x)
    return p
def back(rng, p, share):
    c = np.full((16, W), NV); np.put_along_axis(c, p, np.broadcast_to(np.arange(NV), (16, NV)), 1); mix = rng.random((16, NV))
    return np.where(mix < share, c[:, :NV], np.where(mix < share + 0.03, rng.integers(0, NV, (16, NV)), NV))
def presence(rng, extra):
    h = np.ones(NV, bool); h[:S] = rng.random(S) > 0.01; h[NV - TOP:] = rng.random(TOP) < 0.2; h[S:NV - TOP] = False
    h[S:NV - TOP] = rng.permutation(M) < LIM + extra - int(np.sum(h))
    return h
def parity(rng):
    return 2 * rng.integers(0, 8, (16, NV)) + rng.integers(0, 2, (1, NV))
def start(rng):
    y = rng.integers(0, 16, (N, 8, 16, NV)); m = rng.integers(0, 2, (N, 8, NV)); b = np.argsort(rng.random((N, 8, NV)), axis=-1)[..., :(N - 1) * G].copy()
    y = np.where(rng.random((N, 8, 1, NV)) < 0.15, 2 * (y >> 1) + rng.integers(0, 2, (N, 8, 1, NV)), y)
    p = np.zeros((N, 8, 16, NV), np.int64); c = p.copy(); h = np.zeros((N, 8, NV), bool)
    for q in range(N):
        for g in range(8):
            p[q, g] = layered(rng, FANS); c[q, g] = back(rng, p[q, g], float(rng.choice(np.array([0.5, 0.8, 0.95]))))
            h[q, g] = presence(rng, int(rng.choice(np.array([-60, 0, 40, 120, K2, 2 * K2]))))
    return y, p, c, m, b, h
def pack(y, p, c, m, b, h):
    y = np.where(h[:, :, None, :], y, -1)
    return {"y0": np.ascontiguousarray(y.reshape(N, 128, NV)).astype(np.float32).astype(BF), "pr": np.ascontiguousarray(p.reshape(N, 128, NV)).astype(np.int32), "co": np.ascontiguousarray(c.reshape(N, 128, NV)).astype(np.int32),
            "mo": np.ascontiguousarray(m).astype(np.int32), "bd": np.stack([gtable(a) for a in b])}
def setup_inputs(rng):
    return pack(*start(rng))
def setup_inputs_spread(rng):
    y, p, c, m, b, h = start(rng)
    y = (rng.random((N, 8, 16, NV)) * rng.choice(np.array([1, 2, 3, 8, 16]), (N, 8, 1, NV))).astype(np.int64); y = np.where(rng.random((N, 8, 1, NV)) < 0.5, 15 - y, y)
    m = (rng.random((N, 8, NV)) < rng.choice(np.array([0.03, 0.5, 0.97]), (N, 8, 1))).astype(np.int64)
    for q in range(N):
        for g in range(1, 8, 2):
            o = rng.permutation(NV); im = rng.permutation(W)[:NV]
            p[q, g] = wire(rng, [(o[i:i + 64], im[i:i + 64], int(rng.choice(np.array([2, 2, 3, 5, 16])))) for i in range(0, NV, 64)])
            c[q, g] = np.where(rng.random((16, NV)) < rng.random((1, NV)) * 0.4, rng.integers(0, NV, (16, NV)), NV)
            h[q, g] = rng.random(NV) < float(rng.choice(np.array([0.1, 0.5, 0.8, 0.95])))
    return pack(y, p, c, m, b, h)
def setup_inputs_ends(rng):
    y, p, c, m, b, h = start(rng)
    kind = rng.integers(0, 5, (N, 8, 1, NV)); one = np.arange(16)[:, None] == rng.integers(0, 16, (N, 8, 1, NV)); rnd = rng.random((N, 8, 16, NV)) < 0.75
    odd = np.where(kind == 0, True, np.where(kind == 1, ~one, np.where(kind == 2, one, rnd)))
    y = np.where(odd, 15, 0); y[:, :, :, 1] = 15; y[:, :, :, 2] = 0
    B = (N - 1) * G // 2; both = np.concatenate([np.arange(B), np.arange(NV - B, NV)])
    for q in range(N):
        for g in range(8):
            pp, hh = p[q, g], h[q, g]; b[q, g] = rng.permutation(both)
            if g == 6: hh[:] = True
            if g == 4:
                hh[:] = True; hh[S:NV - TOP] = rng.permutation(M) < LIM + K2 * RO - 1 - S - TOP
                own = [S + int(v) for v in np.nonzero(hh[S:NV - TOP])[0][:8]]
                for i in range(8):
                    v = own[i]; m[q, g, v] = 1; y[q, g, :, v] = np.where(np.arange(16) <= i, 15, 0)
                    for k in range(16): aim(pp, k, v, v if k == (2 * i + 1) % 16 else 16 + i + 8 * (k % 2))
            if g == 2:
                hh[:] = False; hh[:S] = q % 2 == 0
                if q % 2 == 1: pp[:] = sweep(rng, q % 4 == 3)
            if g not in (2, 4, 6): hh[1] = True; hh[2] = True; hh[NV - 1] = False
            if g % 2 == 1: hh[0] = False; hh[NV - 2] = False; aim(pp, 0, 0, 0); aim(pp, 1, NV - 2, 0)
            for k in range(16): aim(pp, k, NV - 1, 1 + k % 2)
            aim(pp, 15, NV - 3, W - 1)
            z = rng.random((1, NV)); mix = np.where(rng.random((16, NV)) < 0.5, 0, NV)
            c[q, g] = np.where(z < 0.5, NV, np.where(z < 0.75, mix, np.where(z < 0.8, 0, back(rng, pp, 0.95))))
            c[q, g, :, 0] = NV; c[q, g, :, NV - 1] = 0
    return pack(y, p, c, m, b, h)
def setup_inputs_corners(rng):
    y, p, c, m, b, h = start(rng); fixed = np.concatenate([np.arange(S), np.arange(NV - TOP, NV)])
    for q in range(N):
        for g in range(8):
            pp, hh = p[q, g], h[q, g]
            if g < 3:
                dl = (g + q) % 3 - 1; hh[:] = True; m[q, g] = 0
                ta = NV - TOP + 1 + rng.permutation(TOP - 2)[:TOP - 18]; nb = K + dl - (TOP - 17); bs = S + rng.permutation(M)[:nb]; na = len(ta)
                hh[ta] = False; hh[bs] = False; hh[NV - TOP] = False; hh[NV - 1] = False
                for j in range(max(na, nb)): aim(pp, j // min(na, nb), int(ta[j % na]), int(bs[j % nb]))
                for k in range(16):
                    aim(pp, k, NV - TOP, 16 + k); aim(pp, k, NV - 1, NV - TOP if k == 0 else k)
                c[q, g] = back(rng, pp, 0.1); c[q, g, 15] = np.where(rng.random(NV) < 0.5, NV - 1, NV)
            if g == 3:
                y[q, g] = parity(rng); hh[:] = True; hh[S:NV - TOP] = rng.permutation(M) < LIM + K2 * RO - 1 + q % 2 - S - TOP
                c[q, g] = NV; b[q, g] = rng.permutation(fixed)[:(N - 1) * G]
            if g == 4:
                y[q, g] = parity(rng); hh[:] = True; hh[S:NV - TOP] = rng.permutation(M) < LIM + q % 4 - S - TOP
                b[q, g] = rng.permutation(fixed)[:(N - 1) * G]
            if g == 5: hh[:] = False; hh[:S] = q % 2 == 1
            if g == 6:
                for i in range(8): aim(pp, i, NV - 1 - i, NV - 1 - i); hh[NV - 1 - i] = False
                z = rng.integers(0, 4, (1, NV)); last = np.where(np.arange(16)[:, None] == 15, NV - 1, NV)
                c[q, g] = np.where(z == 0, NV - 1, np.where(z == 1, last, np.where(z == 2, np.arange(NV)[None, :], NV)))
            if g == 7:
                p[q, g] = layered(rng, np.array([1, 16])); c[q, g] = back(rng, p[q, g], 0.9); h[q, g] = presence(rng, 0)
    return pack(y, p, c, m, b, h)
def setup_inputs_calm(rng):
    y, p, c, m, b, h = start(rng)
    for q in range(N):
        for g in range(6):
            few = (g + q) % 4; pp, hh = p[q, g], h[q, g]; y[q, g] = parity(rng); hh[:] = True
            for t in range(RO):
                for i in range(few):
                    v = NV - 1 - (4 * t + i); hh[v] = False
                    for k in range(16): aim(pp, k, v, v + 4 if k == 0 and t > 0 else 16 + 4 * t + i + 32 * (k % 2))
            hh[S:NV - TOP] = rng.permutation(M) < LIM - S - (TOP - few * RO)
            c[q, g] = NV; c[q, g, 15] = np.where(rng.random(NV) < 0.3, NV - 1 - 4 * (RO - 1), NV); c[q, g, 0] = np.where(rng.random(NV) < 0.2, NV - 5, NV)
            b[q, g] = rng.permutation(np.concatenate([np.arange(S), np.arange(NV - TOP, NV - 4 * RO)]))[:(N - 1) * G]
        pp, hh = p[q, 6], h[q, 6]; y[q, 6] = parity(rng); u = S + (ST * (RO - 1)) % M; x = NV - RO
        o = np.setdiff1d(np.arange(S, NV - TOP), np.array([u])); hh[:] = True; hh[x:] = False; hh[S:NV - TOP] = False
        hh[rng.permutation(o)[:LIM - S - (TOP - RO)]] = True
        for i in range(RO + 1):
            v = NV - 1 - i if i < RO else u
            for k in range(16):
                a = 16 + i + 32 * (k % 2)
                if k == 0 and 0 < i < RO - 1: a = NV - i
                if k == 0 and i == RO - 1: a = u
                if k == 1 and i == RO - 1: a = NV + 2 * G
                if k == 0 and i == RO: a = NV - RO + 1
                aim(pp, k, v, a)
        c[q, 6] = NV; c[q, 6, 3] = np.where(rng.random(NV) < 0.3, x, NV); c[q, 6, :, u] = NV
        b[q, 6] = rng.permutation(np.concatenate([np.arange(S), np.arange(NV - TOP, x)]))[:(N - 1) * G]; b[q, 6, 2 * G] = u
    return pack(y, p, c, m, b, h)
def setup_inputs_crowd(rng):
    y, p, c, m, b, h = start(rng)
    for q in range(N):
        for g in range(8):
            if g % 4 == 0: p[q, g] = layered(rng, np.array([1]))
            if g % 4 == 1: p[q, g] = layered(rng, np.array([16])); h[q, g] = presence(rng, -60); h[q, g, :S] = True
            if g % 4 > 1:
                h[q, g] = rng.random(NV) < 0.8; h[q, g, :S] = True; h[q, g, NV - TOP:] = False; bs = S + rng.permutation(M)[:2 * TOP]
            if g % 4 == 2:
                p[q, g] = flat(rng, np.arange(S)); h[q, g, bs[:TOP]] = False
                for i in range(TOP): aim(p[q, g], i % 16, NV - TOP + i, int(bs[i]))
            if g % 4 == 3:
                p[q, g] = flat(rng, bs); h[q, g, bs] = False
                for i in range(0, TOP, 2): aim(p[q, g], (i >> 1) % 16, NV - TOP + i, i)
            z = rng.random((1, NV)); last = np.where(np.arange(16)[:, None] == 15, NV - 1, NV)
            c[q, g] = np.where(z < 0.2, NV - 1, np.where(z < 0.4, last, back(rng, p[q, g], 0.6)))
    return pack(y, p, c, m, b, h)
def check_inputs(d):
    bad = []
    for k, lo, hi in (("y0", -1, 15), ("pr", 0, W - 1), ("co", 0, NV), ("mo", 0, 1), ("bd", 0, NV - 1)):
        a = np.asarray(d[k]).astype(np.float64)
        if not (np.min(a) >= lo and np.max(a) <= hi): bad.append("range of " + k)
    y = np.asarray(d["y0"]).astype(np.float32).reshape(N, 8, 16, NV); h = y < 0
    if np.any(y != np.floor(y)): bad.append("whole numbers of y0")
    if np.any(np.any(h, axis=2) != np.all(h, axis=2)): bad.append("absent in all 16 branches or in none, of y0")
    s = np.sort(np.asarray(d["pr"]), axis=2)
    if np.any(s[:, :, 1:] == s[:, :, :-1]): bad.append("different numbers in a row of pr")
    s = np.sort(np.stack([gentries(a) for a in np.asarray(d["bd"])]), axis=2)
    if np.any(s[:, :, 1:] == s[:, :, :-1]): bad.append("different entries of a group of bd")
    return bad
def ghosts(y, bl):
    s = np.zeros((N, 8, 16, (N - 1) * G), np.int64)
    for r in range(N):
        for d in range(1, N):
            q = r ^ d; h = twin(d)
            s[r, :, :, (d - 1) * G:d * G] = np.take_along_axis(y[q][h], bl[q][h, d - 1][:, None, :], 2)
    return s
def reference(y0, pr, co, mo, bd):
    y = y0.astype(np.float32).astype(np.int64).reshape(N, 8, 16, NV); ph = np.zeros((N, 8, 16, NV), np.int64)
    p = pr.astype(np.int64).reshape(N, 8, 16, NV); c = co.astype(np.int64).reshape(N, 8, 16, NV); m = mo.astype(np.int64)
    bl = np.stack([gentries(a) for a in bd]).astype(np.int64).reshape(N, 8, N - 1, G)
    want = (y[:, :, 0] < 0) & (np.arange(NV) >= NV - TOP)
    for t in range(RO):
        gh = ghosts(y, bl); a = np.concatenate([y, gh], axis=3)
        tl = np.argsort(~want, axis=2, kind="stable")[..., :K]; live = np.take_along_axis(want, tl, 2)
        pt = np.take_along_axis(p, tl[:, :, None, :], 3)
        v = np.take_along_axis(a, pt.reshape(N, 8, 1, 16 * K), 3).reshape(N, 8, 16, 16, K)
        gone = v[:, :, 0] < 0; diff = np.max(v, axis=3) - np.min(v, axis=3); named = np.zeros((N, 8, W), bool)
        i, j, k, s = np.nonzero(gone & live[:, :, None, :]); named[i, j, pt[i, j, k, s]] = True
        i, j, s = np.nonzero(live & ~np.any(gone, axis=2)); u = tl[i, j, s]
        y[i, j, :, u] = diff[i, j, :, s]; ph[i, j, :, u] = 0
        want = want | named[:, :, :NV]; want[i, j, u] = False
        here = y[:, :, 0] >= 0; e = np.clip(np.add.reduce(here.astype(np.int64), axis=2) - LIM, 0, K2)
        ring = S + (np.arange(M) + ST * t) % M
        rl = ring[np.argsort(~here[:, :, ring], axis=2, kind="stable")[..., :K2]]; live = np.take_along_axis(here, rl, 2)
        wx = np.concatenate([want, np.zeros((N, 8, 1), bool)], axis=2)
        ct = np.take_along_axis(c, rl[:, :, None, :], 3).reshape(N, 8, 16 * K2)
        held = np.any(np.take_along_axis(wx, ct, 2).reshape(N, 8, 16, K2), axis=2)
        fr = (live & ~held).astype(np.int64); go = (fr == 1) & (np.add.accumulate(fr, axis=2) - fr < e[:, :, None])
        has = np.concatenate([here, gh[:, :, 0] >= 0], axis=2); pt = np.take_along_axis(p, rl[:, :, None, :], 3).reshape(N, 8, 16 * K2)
        dirty = ~np.all(np.take_along_axis(has, pt, 2).reshape(N, 8, 16, K2), axis=2)
        old = np.take_along_axis(y, rl[:, :, None, :], 3)
        f = np.where(dirty[:, :, None, :], (old & 1) * np.take_along_axis(m, rl, 2)[:, :, None, :], 0); cnt = np.add.reduce(f, axis=2)
        i, j, s = np.nonzero(go); u = rl[i, j, s]
        ph[i, j, :, u] = f[i, j, :, s]; y[i, j, :, u] = -1
        want[i, j, u] = (cnt[i, j, s] >= 1) & (cnt[i, j, s] <= 15)
        lost = y[:, :, 0] < 0
        for r in range(N):
            for d in range(1, N):
                q = r ^ d; h = twin(d)[:, None]; ix = bl[q][twin(d), d - 1]
                want[q, h, ix] = want[q, h, ix] | (named[r, :, NV + (d - 1) * G:NV + d * G] & lost[q][h, ix])
    return {"yy": y.reshape(N, 128, NV).astype(np.float32).astype(BF), "yf": ph.reshape(N, 128, NV).astype(np.float32).astype(BF), "yw": want.astype(np.float32).astype(BF)}

@@ -1,0 +1,495 @@
+from concourse.bass import DstId, RemoteDMATransfer
+from concourse.mybir import AluOpType as A, ActivationFunctionType as F
+
+NV, S0, TOP, GH, K, LIM, ST, RO = 1536, 384, 192, 32, 192, 704, 432, 3
+RING = NV - S0 - TOP
+NG = 7 * GH
+WD = NV + NG
+WY = WD + K
+NX = NV + K
+CH = 768
+B16, F32, I32, U16 = "bfloat16", "float32", "int32", "uint16"
+
+
+def sb(n, d):
+    return ("sbuf", [128, n], d)
+
+
+SCRATCH = {
+    "Y": sb(WY, B16), "PR": sb(NX, I32), "CO": sb(NX, I32), "MO": sb(NX, I32), "BD": sb(16, I32), "BDu": sb(16, U16),
+    "ZC": sb(440, F32), "V": sb(3072, B16), "SA": sb(3072, B16), "SB": sb(3072, B16), "DG": sb(3072, B16), "HG": sb(3072, B16),
+    "M0": sb(CH, B16), "M64": sb(CH, B16), "MCA": sb(12 * 108, B16), "MCB": sb(12 * 72, B16),
+    "FC": sb(12 * 108, B16), "FS": sb(12 * 108, B16), "R": sb(NX, B16), "HR": sb(RING + K, B16), "RW": sb(112, F32),
+    "F2": sb(K, B16), "Bu": sb(16, U16), "BA": sb(16, B16), "BB": sb(16, B16), "BC": sb(16, B16),
+    "TL0": sb(16, U16), "TLu": sb(16, U16), "RLu": sb(16, U16), "SEL": sb(16, U16),
+    "PTu": sb(K, U16), "PT2": sb(K, U16), "CTu": sb(K, U16), "TU": sb(K, U16), "P": sb(208, F32), "TT": sb(384, F32),
+    "OLD": sb(K, B16), "OL2": sb(K, B16), "Qm": sb(K, B16), "NEW": sb(K, B16), "OI": sb(K, I32), "OM": sb(K, B16),
+    "Ff": sb(K, B16), "F4": sb(K, B16), "A1": sb(K, B16), "AB": sb(K, B16), "RWn": sb(K, B16), "FR": sb(K, B16),
+    "Q": sb(208, B16), "GO": sb(K, B16), "TA": sb(K, B16), "EB": sb(K, B16), "JK": sb(K, B16), "NF": sb(NG, B16), "NT": sb(NG, B16),
+    "ONE": sb(K, B16), "BIG": sb(K, F32), "I16": sb(K, F32), "I1": sb(K, B16), "X0": sb(K, F32),
+    "IP": sb(4, I32), "IM": sb(144, F32), "IG": sb(128, F32), "J": sb(12, F32), "SL": sb(12, F32), "CI": sb(64, I32), "CF": sb(96, F32),
+    "Id": sb(128, B16), "N1": sb(128, B16), "N2": sb(128, B16), "N7": sb(128, B16), "P1": sb(128, B16), "P2": sb(128, B16),
+    "N4": sb(128, B16), "SH": sb(12, F32), "BS": sb(12, F32), "BO": sb(128, B16), "XB": sb(144, B16), "CB": sb(32, F32), "OY": sb(NV, B16), "OF": sb(NV, B16),
+}
+for _t in range(RO + 1):
+    SCRATCH["W%d" % _t] = sb(WY, B16)
+    SCRATCH["G%d" % _t] = sb(NG, B16)
+for _t in range(RO):
+    SCRATCH["Z%d" % _t] = sb(WY, F32)
+    for _n in ("NS", "LG", "LN"):
+        SCRATCH["%s%d" % (_n, _t)] = sb(NG, B16)
+BANKS = ["m0", "m1", "m2", "pa", "pb", "pc", "pd", "ph"]
+for _n in BANKS:
+    SCRATCH[_n] = ("psum", [128, 512], F32)
+
+SEMAPHORES = (["qV", "qA", "qP", "qG", "ly", "lb", "lt", "lp", "lc", "lm", "z1", "z2", "s0", "s1", "s2", "s3", "s4", "s5", "s6"]
+              + ["%s%d" % (n, t) for n in ("ag", "an", "og", "on") for t in range(RO)])
+
+NA = (12, 10, 10)
+PRE_A, PRE_V = 5, 4
+GAP = (0, 1, 1)
+DV = (0, 0, 0)
+DFIRST = (True, False, False)
+EARLY = (1, 4, 6)
+HV = (((0, 64, 64), (64, 128, 128), (128, 140, 192)), ((0, 30, 64), (64, 94, 128), (128, 156, 192)), ((0, 30, 64), (64, 94, 128), (128, 156, 192)))
+CA = 4
+SAME_QUEUE_WAW = True
+
+
+def build(g, core, T, topo):
+    rank = T.rank_of(core)
+    ops = []
+    Q = {"V": g.vector, "A": g.scalar, "P": g.tensor, "G": g, "S": g.sync}
+
+    def r(name, a=None, b=None, s=None):
+        t = T[name]
+        a = 0 if a is None else a
+        b = t.shape[1] if b is None else b
+        return (t[:, a:b] if s is None else t[:, a:b:s], [(name, a, b)], [])
+
+    def ind(name, b, off, c, d):
+        return (T[name][:, 0:b].indirect(T[off][:, c:d]), [(name, 0, b)], [(off, c, d)])
+
+    def op(q, fn, out, ins, sem=None, inc=True, cnt=16):
+        rd = []
+        for x in ins:
+            if isinstance(x, tuple):
+                rd += x[1] + x[2]
+        wr = []
+        if out is not None:
+            wr = out[1]
+            rd += out[2]
+        ops.append({"q": q, "fn": fn, "rd": rd, "wr": wr, "sem": sem, "inc": inc, "cnt": cnt})
+
+    def v(x):
+        return x[0] if isinstance(x, tuple) else x
+
+    def copy(o, i):
+        op("V", lambda: g.vector.tensor_copy(o[0], i[0]), o, [i])
+
+    def tt(o, a, b, f):
+        op("V", lambda: g.vector.tensor_tensor(o[0], a[0], b[0], f), o, [a, b])
+
+    def ts(o, a, s1, f1, s2=None, f2=None):
+        if f2 is None:
+            op("V", lambda: g.vector.tensor_scalar(o[0], a[0], v(s1), None, f1), o, [a, s1])
+        else:
+            op("V", lambda: g.vector.tensor_scalar(o[0], a[0], v(s1), v(s2), f1, f2), o, [a, s1, s2])
+
+    def scan(o, a, b, f1, f2):
+        op("V", lambda: g.vector.tensor_tensor_scan(o[0], a[0], b[0], 0.0, f1, f2), o, [a, b])
+
+    def fill(o, c):
+        op("V", lambda: g.vector.memset(o[0], c), o, [])
+
+    def tr(o, i):
+        op("V", lambda: g.vector.transpose(o[0], i[0]), o, [i])
+
+    def act(o, i, f, bias=0.0, scale=1.0, acc=None):
+        oo = o if acc is None else (o[0], o[1] + acc[1], o[2])
+        if acc is None:
+            op("A", lambda: g.scalar.activation(o[0], i[0], f, bias=v(bias), scale=v(scale)), oo, [i, bias, scale])
+        else:
+            op("A", lambda: g.scalar.activation(o[0], i[0], f, bias=v(bias), scale=v(scale), accum_out=acc[0]), oo, [i, bias, scale])
+
+    def mm(o, l, x, start, stop, inc=None):
+        op("P", lambda: g.tensor.matmul(o[0], l[0], x[0], start, stop), o, [l, x], inc=stop if inc is None else inc)
+
+    def iota(o, pat, base, cm=0):
+        if SCRATCH[o[1][0][0]][2] == I32:
+            op("G", lambda: g.iota(o[0], pat, base, cm), o, [])
+        else:
+            op("G", lambda: g.iota(o[0], pat, base, cm, allow_small_or_imprecise_dtypes=True), o, [])
+
+    def dma(q, o, i, sem, extra=()):
+        op(q, lambda: Q[q].dma_start(o[0], i[0]), o, [i] + list(extra), sem=sem)
+
+    def hbm(ap):
+        return (ap, [], [])
+
+    def send(src, dst, arr, out):
+        def fn():
+            trs = []
+            for d in range(1, len(T.cores)):
+                to = T.cores[rank ^ d]
+                rid, pid = topo.addr(to)[:2]
+                eng = topo.engines(core, to)
+                trs.append(RemoteDMATransfer(dst_ids=[DstId(rid=rid, pnc=pid)], dma_engine_mask=1 << eng[(d - 1) % len(eng)],
+                                             remote_sem=T.sem[arr], src=T[src][:, (d - 1) * GH:d * GH], dst=T[dst][:, (d - 1) * GH:d * GH]))
+            g.remote_dma_fused(trs, local_sem=T.sem[out])
+            return None
+        op("G", fn, (None, [("sent" + out, 0, 1)], []), [r(src)], sem=out, cnt=7)
+        op("X", None, r(dst), [], sem=arr, cnt=7)
+
+    def col(name, j):
+        return r(name, j, j + 1)
+
+    perm = ("P1", "P2", "Id")
+
+    dma("S", r("Y", 0, NV), hbm(T.y0[:, :]), "ly")
+    dma("A", r("BD", 0, 14), hbm(T.bd[:, :]), "lb")
+    dma("A", r("PR", NV - TOP, NV), hbm(T.pr[:, NV - TOP:NV]), "lt")
+    dma("S", r("PR", 0, NV - TOP), hbm(T.pr[:, 0:NV - TOP]), "lp")
+    dma("S", r("CO", 0, NV), hbm(T.co[:, :]), "lc")
+    iota(col("IP", 0), [[0, 1]], 0, 1)
+    iota(r("J"), [[16, 12]], 0)
+    iota(r("PR", NV, NX), [[1, K]], WD)
+    iota(r("IM"), [[1, 144]], 0)
+    iota(r("IG"), [[16, 8], [0, 16]], 0)
+    fill(r("ZC"), 3.0)
+    for i in range(4):
+        act(r("Z0", 440 * i, 440 * (i + 1)), r("ZC"), F.Copy)
+    fill(r("BIG"), 2.13)
+    fill(r("ONE"), 1.0)
+    ci = lambda j, n=1: r("CI", 4 * j, 4 * j + n)
+    cf = lambda j, n=1: r("CF", 4 * j, 4 * j + n)
+    ts(ci(0), col("IP", 0), 15, A.bitwise_and)
+    ts(ci(1), col("IP", 0), 16, A.bitwise_and)
+    ts(ci(2), col("IP", 0), 4, A.arith_shift_right)
+    copy(cf(0), col("IP", 0))
+    fill(r("W0", 0, NV - TOP), 0.0)
+    copy(cf(1), ci(0))
+    copy(cf(2), ci(1))
+    ts(ci(3), ci(2), -1.0, A.mult, 8.0, A.add)
+    fill(r("W0", NV, WY), 0.0)
+    ts(r("SL"), r("J"), cf(1), A.add)
+    ts(ci(4), ci(3), 7, A.bitwise_and)
+    ts(cf(3), cf(0), cf(1), A.subtract)
+    fill(r("Y", WD, WY), -1.0)
+    ts(cf(8, 12), r("SL"), 1.0 / 12, A.mult, 0.5 / 12 - 0.5, A.add)
+    ts(r("TL0", 0, 12), r("SL"), float(NV - TOP), A.add)
+    ts(cf(16, 12), r("SL"), 32.0, A.mult, cf(2), A.add)
+    copy(ci(8, 12), cf(8, 12))
+    ts(cf(4), ci(4), 16.0, A.mult, cf(1), A.add)
+    ts(cf(5), cf(3), -1.0, A.mult, 112.0, A.add)
+    ts(cf(12, 12), ci(8, 12), -383.0, A.mult)
+    copy(r("BDu", 0, 14), r("BD", 0, 14))
+    ts(cf(6), cf(5), cf(1), A.add)
+    tt(cf(20, 12), cf(12, 12), cf(16, 12), A.add)
+    tt(r("X0"), r("PR", NV - TOP, NV), r("PR", NV, NX), A.subtract)
+    copy(r("SEL", 0, 12), cf(20, 12))
+
+    def border(t):
+        act(r("G%d" % t), ind("Y", NV, "BDu", 0, 14), F.Copy)
+
+    def lists():
+        copy(r("P", K, K + 16), r("P", 0, 16))
+        tr(r("TT", 0, K), r("P", 0, K))
+        tr(r("TT", K, 2 * K), r("P", 16, K + 16))
+        copy(r("TU"), ind("TT", 2 * K, "SEL", 0, 12))
+
+    def compact(nb, mask, out, bases, gap, na=0):
+        nv = 12 - na
+        ends = r("R", 15, 16 * nb, 16)
+        for a in range(16):
+            mm(r("pb", 0, nb), r("XB", 15 - a, 143 - a), r("R", a, 16 * nb, 16), a == 0, a == 15)
+        for b in range(nv, 12):
+            act(r("JK", 0, nb) if b % 2 else r("AB", 0, nb), ends, F.Sign, bias=col("SH", b), scale=-1.0, acc=col("BS", b))
+        for b in range(nv):
+            ts(r("FC", b * nb, (b + 1) * nb), ends, col("SL", b), A.is_le)
+        if na:
+            act(r("RW", 0, nb), r("pb", 0, nb), F.Copy)
+        else:
+            copy(r("RW", 0, nb), r("pb", 0, nb))
+        scan(r("FS", 0, nv * nb), r(mask, 0, nv * nb), r("FC", 0, nv * nb), A.mult, A.add)
+        bl = r("FS", nb - 1, nv * nb, nb)
+        if na:
+            ts(r("Bu", nv, 12), r("BS", nv, 12), 0.5, A.mult, nb / 2, A.add)
+        copy(r("Bu", 0, nv), bl)
+        if na:
+            act(r("BA", nv, 12), r("BS", nv, 12), F.Identity, bias=8.0 * nb, scale=8.0)
+            act(r("BA", 0, nv), bl, F.Identity, scale=16.0)
+        tt(r("F2"), ind("RW", nb, "Bu", 0, 12), r("I16"), A.is_le)
+        bs = bases(bl)
+        for a in range(16):
+            mm(r("pc", 0, 12), r("XB", 15 - a, 143 - a), r("F2", a, K, 16), a == 0, False)
+        for i in range(len(bs)):
+            mm(r("pc", 0, 12), r("Id"), bs[i], False, i == len(bs) - 1)
+        gap()
+        copy(r(out, 0, 12), r("pc", 0, 12))
+
+    def ksum(bank, src, a, b):
+        for k in range(16):
+            mm(r(bank, a, b), r("Id"), r(src, 16 * a + k, 16 * b, 16), k == 0, k == 15)
+
+    for t in range(RO):
+        W, Wn, Z = "W%d" % t, "W%d" % (t + 1), "Z%d" % t
+        todo = {"A": list(range(NA[t])), "V": list(range(NA[t], 16))}
+
+        def name(q, n, todo=todo, W=W, Z=Z):
+            for _ in range(n):
+                if todo[q]:
+                    k = todo[q].pop(0)
+                    if q == "A":
+                        o = ind(Z, WY, "TU", 12 * k, 12 * k + 12)
+                        op("A", lambda o=o: g.scalar.activation(o[0], T.BIG[:, :], F.Silu), o, [r("BIG")])
+                    else:
+                        copy(ind(W, WY, "TU", 12 * k, 12 * k + 12), r("ONE"))
+
+        if t == 0:
+            tl = "TL0"
+            border(0)
+            send("G0", "LG0", "ag0", "og0")
+            ts(r("W0", NV - TOP, NV), r("Y", NV - TOP, NV), 0.0, A.is_lt)
+            act(r("SA", 0, NV), r("Y", 0, NV), F.Sign, bias=0.5, acc=col("CB", 28))
+            tt(r("X0"), r("X0"), r("W0", NV - TOP, NV), A.mult)
+            ts(r("Id"), r("IM", 0, 128), cf(0), A.is_equal)
+            tt(r("P", 0, K), r("X0"), r("PR", NV, NX), A.add)
+            ts(r("P1"), r("IM", 0, 128), cf(6), A.is_equal)
+            lists()
+            copy(r("PTu"), r("P", 0, K))
+            ts(r("P2"), r("IM", 0, 128), cf(4), A.is_equal)
+            name("A", PRE_A)
+            fill(r("M0"), 1.0)
+            fill(r("M64"), 0.0)
+            ts(r("N1"), r("Id"), -1.0, A.mult)
+            ts(r("N2"), r("Id"), -2.0, A.mult)
+            ts(r("N7"), r("Id"), -1.75, A.mult)
+            ts(r("N4"), r("Id"), -0.25, A.mult)
+            ts(r("SH"), r("SL"), 0.5, A.add)
+            ts(r("M0", 0, CH, 16), r("ONE", 0, CH // 16), 0.0, A.mult)
+            ts(r("M64", 0, CH, 16), r("ONE", 0, CH // 16), 64.0, A.mult)
+            ts(r("BO"), r("IG"), cf(3), A.is_equal)
+            ts(r("XB"), r("IM"), cf(3), A.subtract, 15.0, A.is_equal)
+            ts(col("CB", 0), col("CB", 28), 0.5, A.mult, float(NV // 2 - LIM), A.add)
+            name("V", PRE_V)
+            iota(r("I16"), [[16, K]], 0)
+            iota(r("HR", RING, RING + K), [[0, K]], 1)
+            iota(r("CO", NV, NX), [[0, K]], WD)
+            iota(r("MO", NV, NX), [[0, K]], 0)
+            iota(r("Q", 0, 16), [[0, 16]], 0)
+            for m, nb in (("MCB", 72), ("MCA", 108)):
+                iota(r(m), [[0, 12 * nb]], 1)
+                op("G", lambda m=m, nb=nb: g.affine_select(T[m][:, :], T[m][:, :], [[0, 12], [1, nb]], A.is_gt, 0.0, 0, 0), r(m), [r(m)])
+                if m == "MCB":
+                    iota(r("W1", NV, WD), [[0, NG]], 0)
+                    iota(r("W1", WD, WY), [[0, K]], 1)
+            iota(r("I1"), [[1, K]], 1)
+            for u in (2, 3):
+                iota(r("W%d" % u, NV, WD), [[0, NG]], 0)
+                iota(r("W%d" % u, WD, WY), [[0, K]], 1)
+            for k in range(16):
+                dma("S", (T.MO[k:128:16, 0:NV], [("MO", 0, NV)], []), hbm(T.mo[:, :]), "lm", [(None, [("sentog0", 0, 1)], [])])
+            for u in (1, 2):
+                for i in range(4):
+                    dma("S", r("Z%d" % u, 440 * i, 440 * (i + 1)), r("ZC"), "z%d" % u)
+        else:
+            tl = "TLu"
+            scan(r("R", 0, NV), r(W, 0, NV), r(W, 0, NV), A.add, A.max)
+            ts(r("R", NV, NX), r("I1"), col("R", NV - 1), A.add)
+            compact(108, "MCA", "TLu", lambda bl: [r("BA", 0, 12)], lambda: None, CA)
+            copy(r("PTu"), ind("PR", NX, "TLu", 0, 12))
+            copy(r("P", 0, K), r("PTu"))
+            lists()
+        for d in range(1, 8):
+            mm(r("pa", (d - 1) * GH, d * GH), r(perm[(d - 1) % 3]), r("LG%d" % t, (d - 1) * GH, d * GH), True, True, inc=d == 7)
+        act(r("Y", NV, WD), r("pa", 0, NG), F.Copy)
+        for c in range(3):
+            act(r("V", CH * c, CH * (c + 1)), ind("Y", WY, "PTu", 48 * c, 48 * (c + 1)), F.Copy)
+        copy(r("V", 3 * CH, 4 * CH), ind("Y", WY, "PTu", 144, 192))
+        act(r("OLD"), ind("Y", WY, tl, 0, 12), F.Copy)
+        for c in (0, 3, 1, 2):
+            a, b = CH * c, CH * (c + 1)
+            scan(r("SB", a, b), r("M64"), r("V", a, b), A.add, A.min)
+            if c == 2:
+                ts(r("Qm"), r("SB", 15, 3072, 16), 0.0, A.is_lt, 64.0, A.mult)
+                mm(r("pa", 0, K), r("N1"), r("SB", 15, 3072, 16), True, False)
+                mm(r("pa", 0, K), r("N1"), r("Qm"), False, False)
+            scan(r("SA", a, b), r("M0"), r("V", a, b), A.mult, A.max)
+        mm(r("pa", 0, K), r("Id"), r("SA", 15, 3072, 16), False, True)
+        name("A", 2)
+        act(r("JK"), r("Qm"), F.Identity, bias=1.0, scale=-1.0 / 64, acc=col("CB", 16 + 4 * t))
+        act(r("EB"), r("ONE"), F.Relu, bias=col("CB", 4 * t), scale=col("CB", 16 + 4 * t))
+        if t + 1 < RO:
+            act(col("CB", 17 + 4 * t), col("CB", 16 + 4 * t), F.Identity, bias=col("CB", 4 * t))
+        tt(r("NEW"), r("OLD"), r("pa", 0, K), A.max)
+        copy(ind("Y", WY, tl, 0, 12), r("NEW"))
+        st = (ST * t) % RING
+        ts(r("HR", 0, RING - st), r("Y", S0 + st, S0 + RING), 0.0, A.is_ge)
+        if st:
+            ts(r("HR", RING - st, RING), r("Y", S0, S0 + st), 0.0, A.is_ge)
+        scan(r("R", 0, RING + K), r("HR"), r("HR"), A.add, A.max)
+
+        def rbase(bl, st=st):
+            ts(r("BA", 0, 12), bl, 16.0, A.mult, float(S0 + st), A.add)
+            if st == 0:
+                ts(r("BB", 0, 12), bl, RING // 16 - 0.5, A.is_ge, float(TOP), A.mult)
+                return [r("BA", 0, 12), r("BB", 0, 12)]
+            ts(r("BB", 0, 12), bl, (RING - st) // 16 - 0.5, A.is_ge, -float(RING), A.mult)
+            ts(r("BC", 0, 12), bl, RING // 16 - 0.5, A.is_ge, float(RING + TOP - st), A.mult)
+            return [r("BA", 0, 12), r("BB", 0, 12), r("BC", 0, 12)]
+        compact(72, "MCB", "RLu", rbase, lambda: name("V", GAP[t]))
+        copy(r("PT2"), ind("PR", NX, "RLu", 0, 12))
+        for j in range(3):
+            mm(r("m%d" % j), r("N2"), r("Y", 512 * j, 512 * (j + 1)), True, False)
+        mm(r("pa", 0, NG), r("N7"), r("G%d" % t), True, False, inc=True)
+        name("A", 16)
+        dv = DV[t]
+        dm = (K - dv) // 4 * 2
+        for a, b in ((0, dm), (dm, K - dv)):
+            act(r("DG", 16 * a, 16 * b), ind("Y", WY, "PT2", a, b), F.Relu, scale=-1.0)
+        act(r("OL2"), ind("Y", WY, "RLu", 0, 12), F.Copy)
+        side = [lambda: copy(r("CTu"), ind("CO", NX, "RLu", 0, 12)), lambda: copy(r("OI"), ind("Y", WY, "RLu", 0, 12)),
+                lambda: ts(r("OI"), r("OI"), 1, A.bitwise_and), lambda: tt(r("OM"), ind("MO", NX, "RLu", 0, 12), r("OI"), A.mult)]
+        if t == RO - 1:
+            side += [lambda: ts(r("OY", 0, S0), r("Y", 0, S0), -1.0, A.max), lambda: ts(r("OY", NV - TOP, NV), r("Y", NV - TOP, NV), -1.0, A.max)]
+        late = side[EARLY[t]:]
+        side = side[:EARLY[t]]
+        for f in side[:-1]:
+            name("V", 1)
+            f()
+        name("V", 16)
+        if t:
+            ksum("pd", "DG", 0, dm)
+        for j in range(3):
+            mm(r("m%d" % j), r("Id"), r(W, 512 * j, 512 * (j + 1)), False, True)
+        side[-1]()
+        mm(r("pc", 0, NG), r("Id"), r(W, NV, WD), True, False)
+        for a in (0, NG // 2):
+            mm(r("pc", a, a + NG // 2), r("N2"), r("Y", WD, WD + NG // 2), False, a > 0)
+        if dv and DFIRST[t]:
+            ts(r("DG", 16 * (K - dv), 16 * K), ind("Y", WY, "PT2", K - dv, K), 0.0, A.is_lt)
+        for j in range(3):
+            tt(r(Wn, 512 * j, 512 * (j + 1)), r("m%d" % j), r(Z, 512 * j, 512 * (j + 1)), A.is_ge)
+        tt(r("NS%d" % t), r("pc", 0, NG), r(Z, NV, WD), A.is_ge)
+        send("NS%d" % t, "LN%d" % t, "an%d" % t, "on%d" % t)
+        if dv and not DFIRST[t]:
+            ts(r("DG", 16 * (K - dv), 16 * K), ind("Y", WY, "PT2", K - dv, K), 0.0, A.is_lt)
+        if t == 0:
+            ksum("pd", "DG", 0, dm)
+        ksum("pd", "DG", dm, K)
+        hw = WD + 16
+        for f in late:
+            f()
+        for i, (a, m, b) in enumerate(HV[t]):
+            if m > a:
+                copy(r("HG", 16 * a, 16 * m), ind(Wn, hw, "CTu", a, m))
+            if b > m:
+                act(r("HG", 16 * m, 16 * b), ind(Wn, hw, "CTu", m, b), F.Copy)
+            if i == len(HV[t]) - 1:
+                mm(r("pb", 0, K), r("BO"), r("Ff"), True, True)
+                mm(r("pd", 0, K), r("N4"), r("Ff"), True, False)
+                mm(r("pd", 0, K), r("N1"), r("OL2"), False, True)
+            ksum("ph", "HG", a, b)
+            if i == len(HV[t]) - 2:
+                tt(r("Ff"), r("OM"), r("pd", 0, K), A.min)
+        act(r("A1"), r("pd", 0, K), F.Identity, bias=-1.0)
+        act(r("AB"), r("pb", 0, K), F.Abs, bias=-8.0)
+        act(r("RWn"), r("AB"), F.Sign, bias=8.0, scale=-1.0)
+        if t == RO - 1:
+            for a, b, s1, s2 in ((0, S0, "s0", "s1"), (NV - TOP, NV, "s2", "s3")):
+                act(r("OF", a, b), r("Y", a, b), F.Relu, bias=-4.0, scale=-4.0)
+                dma("S", hbm(T.yy[:, a:b]), r("OY", a, b), s1)
+                dma("S", hbm(T.yf[:, a:b]), r("OF", a, b), s2)
+        ts(r("FR"), r("ph", 0, K), 0.5, A.is_lt)
+        scan(r("Q", 1, K + 1), r("FR"), r("EB"), A.add, A.min)
+        mm(r("pc", 0, K), r("Id"), r("Q", 1, K + 1), True, False)
+        mm(r("pc", 0, K), r("N1"), r("Q", 0, K), False, True)
+        tt(r("TA"), r("A1"), r("pc", 0, K), A.mult)
+        act(r("GO"), r("pc", 0, K), F.Copy)
+        tt(ind("Y", WY, "RLu", 0, 12), r("TA"), r("OL2"), A.add)
+        border(t + 1)
+        if t + 1 < RO:
+            send("G%d" % (t + 1), "LG%d" % (t + 1), "ag%d" % (t + 1), "og%d" % (t + 1))
+        tt(ind(Wn, WY, "RLu", 0, 12), r("GO"), r("RWn"), A.mult)
+        for d in range(1, 8):
+            mm(r("pa", (d - 1) * GH, d * GH), r(perm[(d - 1) % 3]), r("LN%d" % t, (d - 1) * GH, d * GH), False, False)
+        mm(r("pa", 0, NG), r("N7"), r("G%d" % (t + 1)), False, True)
+        act(r("NF"), r("pa", 0, NG), F.Sign, bias=-4.44)
+        if t + 1 < RO:
+            act(col("CB", 4 * t + 4), col("Q", K), F.Identity, bias=col("CB", 17 + 4 * t), scale=-1.0)
+        else:
+            ts(r("OY", S0, NV - TOP), r("Y", S0, NV - TOP), -1.0, A.max)
+            dma("S", hbm(T.yy[:, S0:NV - TOP]), r("OY", S0, NV - TOP), "s4")
+            act(r("OF", S0, NV - TOP), r("Y", S0, NV - TOP), F.Relu, bias=-4.0, scale=-4.0)
+            dma("A", hbm(T.yf[:, S0:NV - TOP]), r("OF", S0, NV - TOP), "s5")
+        tt(r("NT"), ind(Wn, NV, "BDu", 0, 14), r("NF"), A.max)
+        copy(ind(Wn, NV, "BDu", 0, 14), r("NT"))
+    dma("S", hbm(T.yw[:, :]), (T.W3[0:128:16, 0:NV], [("W3", 0, NV)], []), "s6")
+    return ops, Q
+
+
+def emit(g, T, ops, Q):
+    total = {}
+    for o in ops:
+        if o["sem"] is None:
+            s = "q" + o["q"]
+            total[s] = total.get(s, 0) + (1 if o["inc"] else 0)
+            o["s"], o["n"] = s, total[s] + (0 if o["inc"] else 1)
+        else:
+            total[o["sem"]] = total.get(o["sem"], 0) + o["cnt"]
+    seen = {}
+    known = {q: {} for q in Q}
+    hist = {}
+    for o in ops:
+        q = o["q"]
+        if o["sem"] is not None:
+            o["s"], o["n"] = o["sem"], total[o["sem"]]
+        need = {}
+        for acc, w in [(x, False) for x in o["rd"]] + [(x, True) for x in o["wr"]]:
+            bank = acc[0] in BANKS
+            for a, b, pw, p in hist.get(acc[0], []):
+                if p is o:
+                    continue
+                if bank and p["q"] != q:
+                    hit = True
+                else:
+                    hit = (w or pw) and a < acc[2] and acc[1] < b
+                    if hit and p["q"] == q and p["sem"] is None and o["sem"] is None and (q == "P" or (w and not SAME_QUEUE_WAW)):
+                        hit = False
+                    if hit and p["sem"] is not None and p["sem"] == o["sem"]:
+                        hit = False
+                if hit and need.get(p["s"], (0, None))[0] < p["n"]:
+                    need[p["s"]] = (p["n"], p)
+        if q != "X":
+            kn = known[q]
+            for s in sorted(need, key=lambda s: -need[s][1]["i"]):
+                n, p = need[s]
+                if kn.get(s, 0) < n:
+                    Q[q].wait_ge(T.sem[s], n)
+                    seen[s] = max(seen.get(s, 0), n)
+                    kn[s] = n
+                    for s2, n2 in p["k"].items():
+                        kn[s2] = max(kn.get(s2, 0), n2)
+            ins = o["fn"]()
+            if ins is not None and o["inc"]:
+                ins.then_inc(T.sem[o["s"]], 1 if o["sem"] is None else 16)
+            o["k"] = dict(kn) if o["sem"] is None else {}
+        else:
+            o["k"] = {}
+        o["i"] = len(hist.setdefault("", []))
+        hist[""].append(0)
+        for acc in o["rd"]:
+            hist.setdefault(acc[0], []).append((acc[1], acc[2], False, o))
+        for acc in o["wr"]:
+            hist.setdefault(acc[0], []).append((acc[1], acc[2], True, o))
+    for s in total:
+        if seen.get(s, 0) < total[s]:
+            g.wait_ge(T.sem[s], total[s])
+
+
+def rank_program(g, core, T, topo):
+    if T.rank_of(core) is None:
+        return
+    ops, Q = build(g, core, T, topo)
+    emit(g, T, ops, Q)

@@ -7,8 +7,11 @@ NG = 7 * GH
 WD = NV + NG
 WY = WD + K
 NX = NV + K
-CH = 768
-B16, F32, I32, U16 = "bfloat16", "float32", "int32", "uint16"
+CS = 48
+NBT, NBR = NV // 16, (RING + K) // 16
+B16, F16, F32, I32, U16 = "bfloat16", "float16", "float32", "int32", "uint16"
+EPS = 2.0 ** -9
+ZMARK, ZNONE, WW, WYS = (30, 24, 18), 35.0, 15.5, (30.25, 25.0, 20.0)
 
 
 def sb(n, d):
@@ -17,43 +20,49 @@ def sb(n, d):
 
 SCRATCH = {
     "Y": sb(WY, B16), "PR": sb(NX, I32), "CO": sb(NX, I32), "MO": sb(NX, I32), "BD": sb(16, I32), "BDu": sb(16, U16),
-    "ZC": sb(440, F32), "V": sb(3072, B16), "SA": sb(3072, B16), "SB": sb(3072, B16), "DG": sb(3072, B16), "HG": sb(3072, B16),
-    "M0": sb(CH, B16), "M64": sb(CH, B16), "MCA": sb(12 * 108, B16), "MCB": sb(12 * 72, B16),
-    "FC": sb(12 * 108, B16), "FS": sb(12 * 108, B16), "R": sb(NX, B16), "HR": sb(RING + K, B16), "RW": sb(112, F32),
-    "F2": sb(K, B16), "Bu": sb(16, U16), "BA": sb(16, B16), "BB": sb(16, B16), "BC": sb(16, B16),
-    "TL0": sb(16, U16), "TLu": sb(16, U16), "RLu": sb(16, U16), "SEL": sb(16, U16),
+    "Z": sb(WY, F32), "ZC": sb(WY // 4, F32), "JS": sb(NV, B16),
+    "VA": sb(16 * CS, B16), "SAa": sb(16 * CS, B16), "SBa": sb(16 * CS, B16), "M0": sb(16 * CS, B16), "M1": sb(16 * CS, B16),
+    "VF": sb(16 * K, F16), "SAf": sb(8 * K, F16), "SBf": sb(16 + 8 * K, F16), "OFF": sb(16 * CS, B16),
+    "DG": sb(16 * K, B16), "HG": sb(16 * K, B16),
+    "MCA": sb(12 * NBT, B16), "MCB": sb(12 * NBR, B16), "FC": sb(12 * NBT, B16), "FS": sb(12 * NBT, B16),
+    "R": sb(NV // 2, B16), "HR": sb(RING + K, B16), "RWT": sb(112, F32), "RWR": sb(80, F32),
+    "F2": sb(K, B16), "Bu": sb(16, U16), "BA": sb(16, B16), "BB": sb(16, B16), "BC": sb(16, B16), "BF": sb(16, B16),
+    "TLu": sb(16, U16), "RLu": sb(16, U16), "SEL": sb(16, U16),
     "PTu": sb(K, U16), "PT2": sb(K, U16), "CTu": sb(K, U16), "TU": sb(K, U16), "P": sb(208, F32), "TT": sb(384, F32),
-    "OLD": sb(K, B16), "OL2": sb(K, B16), "Qm": sb(K, B16), "NEW": sb(K, B16), "OI": sb(K, I32), "OM": sb(K, B16),
-    "Ff": sb(K, B16), "F4": sb(K, B16), "A1": sb(K, B16), "AB": sb(K, B16), "RWn": sb(K, B16), "FR": sb(K, B16),
-    "Q": sb(208, B16), "GO": sb(K, B16), "TA": sb(K, B16), "EB": sb(K, B16), "JK": sb(K, B16), "NF": sb(NG, B16), "NT": sb(NG, B16),
-    "ONE": sb(K, B16), "BIG": sb(K, F32), "I16": sb(K, F32), "I1": sb(K, B16), "X0": sb(K, F32),
+    "OLD": sb(K, B16), "OL2": sb(K, B16), "Qm": sb(K, B16), "NEW": sb(K, B16), "OI": sb(K, I32), "OM": sb(K, I32),
+    "Ff": sb(K, B16), "A1": sb(K, B16), "AB": sb(K, B16), "TH": sb(K, B16), "RW2": sb(K, B16), "FR": sb(K, B16),
+    "Q": sb(208, B16), "GO": sb(K, B16), "TA": sb(K, B16), "EB": sb(K, B16), "JK": sb(K, B16), "JL": sb(K, B16),
+    "SG": sb(NG, B16), "NF": sb(NG, B16), "NT": sb(NG, B16),
+    "ONE": sb(K, B16), "BIG": sb(RO * K, F32), "I16": sb(K, F32), "X0": sb(K, F32),
     "IP": sb(4, I32), "IM": sb(144, F32), "IG": sb(128, F32), "J": sb(12, F32), "SL": sb(12, F32), "CI": sb(64, I32), "CF": sb(96, F32),
-    "Id": sb(128, B16), "N1": sb(128, B16), "N2": sb(128, B16), "N7": sb(128, B16), "P1": sb(128, B16), "P2": sb(128, B16),
-    "N4": sb(128, B16), "SH": sb(12, F32), "BS": sb(12, F32), "BO": sb(128, B16), "XB": sb(144, B16), "CB": sb(32, F32), "OY": sb(NV, B16), "OF": sb(NV, B16),
+    "SH": sb(12, F32), "BS": sb(12, F32), "CB": sb(32, F32),
+    "XB": sb(144, B16), "XN": sb(144, B16), "X2": sb(144, B16), "OY": sb(NV, B16), "OF": sb(NV, B16), "OW": sb(NX, B16),
 }
+DIAG = {"Id": 1.0, "N1": -1.0, "N8": -0.125, "N64": -64.0, "NH": -0.5, "NE": EPS / 2, "PW": WW, "Y0": -WYS[0], "Y1": -WYS[1], "Y2": -WYS[2]}
+for _n in list(DIAG) + ["P1", "P2", "BO"]:
+    SCRATCH[_n] = sb(128, B16)
 for _t in range(RO + 1):
     SCRATCH["W%d" % _t] = sb(WY, B16)
-    SCRATCH["G%d" % _t] = sb(NG, B16)
 for _t in range(RO):
-    SCRATCH["Z%d" % _t] = sb(WY, F32)
-    for _n in ("NS", "LG", "LN"):
+    for _n in ("G", "NS", "LG", "LN"):
         SCRATCH["%s%d" % (_n, _t)] = sb(NG, B16)
 BANKS = ["m0", "m1", "m2", "pa", "pb", "pc", "pd", "ph"]
 for _n in BANKS:
     SCRATCH[_n] = ("psum", [128, 512], F32)
 
-SEMAPHORES = (["qV", "qA", "qP", "qG", "ly", "lb", "lt", "lp", "lc", "lm", "z1", "z2", "s0", "s1", "s2", "s3", "s4", "s5", "s6"]
+SEMAPHORES = (["qV", "qA", "qP", "qG", "ly", "lb", "lt", "lp", "lq", "lc", "lm", "s0", "s1", "s2", "s3", "s4", "s5", "s6"]
               + ["%s%d" % (n, t) for n in ("ag", "an", "og", "on") for t in range(RO)])
 
-NA = (12, 10, 10)
-PRE_A, PRE_V = 5, 4
-GAP = (0, 1, 1)
-DV = (0, 0, 0)
-DFIRST = (True, False, False)
-EARLY = (1, 4, 6)
-HV = (((0, 64, 64), (64, 128, 128), (128, 140, 192)), ((0, 30, 64), (64, 94, 128), (128, 156, 192)), ((0, 30, 64), (64, 94, 128), (128, 156, 192)))
-CA = 4
-SAME_QUEUE_WAW = True
+CFG = {
+    "NA": (14, 13, 13),
+    "AV": (1, 1, 1),
+    "PRE": 8,
+    "VE": (0, 1, 1),
+    "CA": 4,
+    "DG": ((0, 64, 128, 192),) * 3,
+    "HG": ((0, 64, 128, 172),) * 3,
+    "FF": (0, 0, 0),
+}
 
 
 def build(g, core, T, topo):
@@ -66,6 +75,10 @@ def build(g, core, T, topo):
         a = 0 if a is None else a
         b = t.shape[1] if b is None else b
         return (t[:, a:b] if s is None else t[:, a:b:s], [(name, a, b)], [])
+
+    def back(name, a, b, s):
+        t = T[name]
+        return (t[:, b - 1::-s] if a == 0 else t[:, b - 1:a - 1:-s], [(name, a, b)], [])
 
     def ind(name, b, off, c, d):
         return (T[name][:, 0:b].indirect(T[off][:, c:d]), [(name, 0, b)], [(off, c, d)])
@@ -96,8 +109,8 @@ def build(g, core, T, topo):
         else:
             op("V", lambda: g.vector.tensor_scalar(o[0], a[0], v(s1), v(s2), f1, f2), o, [a, s1, s2])
 
-    def scan(o, a, b, f1, f2):
-        op("V", lambda: g.vector.tensor_tensor_scan(o[0], a[0], b[0], 0.0, f1, f2), o, [a, b])
+    def scan(o, a, b, f1, f2, init=0.0):
+        op("V", lambda: g.vector.tensor_tensor_scan(o[0], a[0], b[0], init, f1, f2), o, [a, b])
 
     def fill(o, c):
         op("V", lambda: g.vector.memset(o[0], c), o, [])
@@ -112,6 +125,9 @@ def build(g, core, T, topo):
         else:
             op("A", lambda: g.scalar.activation(o[0], i[0], f, bias=v(bias), scale=v(scale), accum_out=acc[0]), oo, [i, bias, scale])
 
+    def silu(o, i):
+        op("A", lambda: g.scalar.activation(o[0], i[0], F.Silu), o, [i])
+
     def mm(o, l, x, start, stop, inc=None):
         op("P", lambda: g.tensor.matmul(o[0], l[0], x[0], start, stop), o, [l, x], inc=stop if inc is None else inc)
 
@@ -120,6 +136,9 @@ def build(g, core, T, topo):
             op("G", lambda: g.iota(o[0], pat, base, cm), o, [])
         else:
             op("G", lambda: g.iota(o[0], pat, base, cm, allow_small_or_imprecise_dtypes=True), o, [])
+
+    def const(o, c):
+        iota(o, [[0, o[1][0][2] - o[1][0][1]]], c)
 
     def dma(q, o, i, sem, extra=()):
         op(q, lambda: Q[q].dma_start(o[0], i[0]), o, [i] + list(extra), sem=sem)
@@ -145,21 +164,22 @@ def build(g, core, T, topo):
         return r(name, j, j + 1)
 
     perm = ("P1", "P2", "Id")
+    top, ring = (NV - TOP, NV), (S0, NV - TOP)
 
     dma("S", r("Y", 0, NV), hbm(T.y0[:, :]), "ly")
     dma("A", r("BD", 0, 14), hbm(T.bd[:, :]), "lb")
-    dma("A", r("PR", NV - TOP, NV), hbm(T.pr[:, NV - TOP:NV]), "lt")
-    dma("S", r("PR", 0, NV - TOP), hbm(T.pr[:, 0:NV - TOP]), "lp")
-    dma("S", r("CO", 0, NV), hbm(T.co[:, :]), "lc")
+    dma("A", r("PR", *top), hbm(T.pr[:, top[0]:top[1]]), "lt")
+    dma("S", r("PR", *ring), hbm(T.pr[:, ring[0]:ring[1]]), "lp", [r("Y", 0, NV)])
     iota(col("IP", 0), [[0, 1]], 0, 1)
     iota(r("J"), [[16, 12]], 0)
-    iota(r("PR", NV, NX), [[1, K]], WD)
     iota(r("IM"), [[1, 144]], 0)
+    iota(r("PR", NV, NX), [[1, K]], WD)
     iota(r("IG"), [[16, 8], [0, 16]], 0)
-    fill(r("ZC"), 3.0)
+    const(r("BIG", 0, K), ZMARK[0])
+    const(r("HR", RING, RING + K), 1)
+    fill(r("ZC"), ZNONE)
     for i in range(4):
-        act(r("Z0", 440 * i, 440 * (i + 1)), r("ZC"), F.Copy)
-    fill(r("BIG"), 2.13)
+        silu(r("Z", WY // 4 * i, WY // 4 * (i + 1)), r("ZC"))
     fill(r("ONE"), 1.0)
     ci = lambda j, n=1: r("CI", 4 * j, 4 * j + n)
     cf = lambda j, n=1: r("CF", 4 * j, 4 * j + n)
@@ -167,30 +187,29 @@ def build(g, core, T, topo):
     ts(ci(1), col("IP", 0), 16, A.bitwise_and)
     ts(ci(2), col("IP", 0), 4, A.arith_shift_right)
     copy(cf(0), col("IP", 0))
-    fill(r("W0", 0, NV - TOP), 0.0)
     copy(cf(1), ci(0))
     copy(cf(2), ci(1))
     ts(ci(3), ci(2), -1.0, A.mult, 8.0, A.add)
-    fill(r("W0", NV, WY), 0.0)
     ts(r("SL"), r("J"), cf(1), A.add)
     ts(ci(4), ci(3), 7, A.bitwise_and)
     ts(cf(3), cf(0), cf(1), A.subtract)
     fill(r("Y", WD, WY), -1.0)
     ts(cf(8, 12), r("SL"), 1.0 / 12, A.mult, 0.5 / 12 - 0.5, A.add)
-    ts(r("TL0", 0, 12), r("SL"), float(NV - TOP), A.add)
     ts(cf(16, 12), r("SL"), 32.0, A.mult, cf(2), A.add)
+    ts(r("Id"), r("IM", 0, 128), cf(0), A.is_equal)
     copy(ci(8, 12), cf(8, 12))
     ts(cf(4), ci(4), 16.0, A.mult, cf(1), A.add)
     ts(cf(5), cf(3), -1.0, A.mult, 112.0, A.add)
     ts(cf(12, 12), ci(8, 12), -383.0, A.mult)
-    copy(r("BDu", 0, 14), r("BD", 0, 14))
+    ts(r("XB"), r("IM"), cf(3), A.subtract, 15.0, A.is_equal)
     ts(cf(6), cf(5), cf(1), A.add)
     tt(cf(20, 12), cf(12, 12), cf(16, 12), A.add)
-    tt(r("X0"), r("PR", NV - TOP, NV), r("PR", NV, NX), A.subtract)
+    ts(r("SH"), r("SL"), 0.75, A.add)
+    copy(r("BDu", 0, 14), r("BD", 0, 14))
+    ts(r("XN"), r("XB"), -1.0, A.mult)
     copy(r("SEL", 0, 12), cf(20, 12))
-
-    def border(t):
-        act(r("G%d" % t), ind("Y", NV, "BDu", 0, 14), F.Copy)
+    fill(r("X2", 143, 144), 0.0)
+    tt(r("X2", 0, 143), r("XB", 0, 143), r("XB", 1, 144), A.add)
 
     def lists():
         copy(r("P", K, K + 16), r("P", 0, 16))
@@ -198,28 +217,30 @@ def build(g, core, T, topo):
         tr(r("TT", K, 2 * K), r("P", 16, K + 16))
         copy(r("TU"), ind("TT", 2 * K, "SEL", 0, 12))
 
-    def compact(nb, mask, out, bases, gap, na=0):
+    def compact(row, nb, mask, rw, out, bases, gap, na=0, mid=None):
         nv = 12 - na
-        ends = r("R", 15, 16 * nb, 16)
-        for a in range(16):
-            mm(r("pb", 0, nb), r("XB", 15 - a, 143 - a), r("R", a, 16 * nb, 16), a == 0, a == 15)
+        for j in range(8):
+            mm(r("pb", 0, nb), r("XN", 15 - 2 * j, 143 - 2 * j), r(row, 2 * j + 1, 16 * nb, 16), j == 0, False)
+        scan(r("R", 0, 8 * nb), r(row, 0, 16 * nb, 2), r(row, 1, 16 * nb, 2), A.add, A.add)
+        ends = r("R", 7, 8 * nb, 8)
+        for j in range(8):
+            mm(r("pb", 0, nb), r("X2", 14 - 2 * j, 142 - 2 * j), r("R", j, 8 * nb, 8), False, j == 7)
+        if mid:
+            mid()
         for b in range(nv, 12):
-            act(r("JK", 0, nb) if b % 2 else r("AB", 0, nb), ends, F.Sign, bias=col("SH", b), scale=-1.0, acc=col("BS", b))
+            act(r("JK" if b % 2 else "JL", 0, nb), ends, F.Sign, bias=col("SH", b), scale=-1.0, acc=col("BS", b))
         for b in range(nv):
-            ts(r("FC", b * nb, (b + 1) * nb), ends, col("SL", b), A.is_le)
+            ts(r("FC", b * nb, (b + 1) * nb), ends, col("SH", b), A.is_le)
         if na:
-            act(r("RW", 0, nb), r("pb", 0, nb), F.Copy)
+            act(r(rw, 0, nb), r("pb", 0, nb), F.Copy)
         else:
-            copy(r("RW", 0, nb), r("pb", 0, nb))
-        scan(r("FS", 0, nv * nb), r(mask, 0, nv * nb), r("FC", 0, nv * nb), A.mult, A.add)
+            copy(r(rw, 0, nb), r("pb", 0, nb))
+        scan(r("FS", 0, nv * nb), r(mask, 0, nv * nb), r("FC", 0, nv * nb), A.min, A.add)
         bl = r("FS", nb - 1, nv * nb, nb)
         if na:
             ts(r("Bu", nv, 12), r("BS", nv, 12), 0.5, A.mult, nb / 2, A.add)
         copy(r("Bu", 0, nv), bl)
-        if na:
-            act(r("BA", nv, 12), r("BS", nv, 12), F.Identity, bias=8.0 * nb, scale=8.0)
-            act(r("BA", 0, nv), bl, F.Identity, scale=16.0)
-        tt(r("F2"), ind("RW", nb, "Bu", 0, 12), r("I16"), A.is_le)
+        tt(r("F2"), ind(rw, SCRATCH[rw][1][1], "Bu", 0, 12), r("I16"), A.is_le)
         bs = bases(bl)
         for a in range(16):
             mm(r("pc", 0, 12), r("XB", 15 - a, 143 - a), r("F2", a, K, 16), a == 0, False)
@@ -228,109 +249,19 @@ def build(g, core, T, topo):
         gap()
         copy(r(out, 0, 12), r("pc", 0, 12))
 
-    def ksum(bank, src, a, b):
-        for k in range(16):
-            mm(r(bank, a, b), r("Id"), r(src, 16 * a + k, 16 * b, 16), k == 0, k == 15)
+    def tbase(bl):
+        ts(r("BA", 0, 12), r("Bu", 0, 12), 16.0, A.mult)
+        ts(r("BF", 0, 12), r("Bu", 0, 12), NBT - 0.5, A.is_ge)
+        tt(r("BB", 0, 12), r("BF", 0, 12), r("SL"), A.mult)
+        return [r("BA", 0, 12), r("BB", 0, 12)]
 
-    for t in range(RO):
-        W, Wn, Z = "W%d" % t, "W%d" % (t + 1), "Z%d" % t
-        todo = {"A": list(range(NA[t])), "V": list(range(NA[t], 16))}
-
-        def name(q, n, todo=todo, W=W, Z=Z):
-            for _ in range(n):
-                if todo[q]:
-                    k = todo[q].pop(0)
-                    if q == "A":
-                        o = ind(Z, WY, "TU", 12 * k, 12 * k + 12)
-                        op("A", lambda o=o: g.scalar.activation(o[0], T.BIG[:, :], F.Silu), o, [r("BIG")])
-                    else:
-                        copy(ind(W, WY, "TU", 12 * k, 12 * k + 12), r("ONE"))
-
-        if t == 0:
-            tl = "TL0"
-            border(0)
-            send("G0", "LG0", "ag0", "og0")
-            ts(r("W0", NV - TOP, NV), r("Y", NV - TOP, NV), 0.0, A.is_lt)
-            act(r("SA", 0, NV), r("Y", 0, NV), F.Sign, bias=0.5, acc=col("CB", 28))
-            tt(r("X0"), r("X0"), r("W0", NV - TOP, NV), A.mult)
-            ts(r("Id"), r("IM", 0, 128), cf(0), A.is_equal)
-            tt(r("P", 0, K), r("X0"), r("PR", NV, NX), A.add)
-            ts(r("P1"), r("IM", 0, 128), cf(6), A.is_equal)
-            lists()
-            copy(r("PTu"), r("P", 0, K))
-            ts(r("P2"), r("IM", 0, 128), cf(4), A.is_equal)
-            name("A", PRE_A)
-            fill(r("M0"), 1.0)
-            fill(r("M64"), 0.0)
-            ts(r("N1"), r("Id"), -1.0, A.mult)
-            ts(r("N2"), r("Id"), -2.0, A.mult)
-            ts(r("N7"), r("Id"), -1.75, A.mult)
-            ts(r("N4"), r("Id"), -0.25, A.mult)
-            ts(r("SH"), r("SL"), 0.5, A.add)
-            ts(r("M0", 0, CH, 16), r("ONE", 0, CH // 16), 0.0, A.mult)
-            ts(r("M64", 0, CH, 16), r("ONE", 0, CH // 16), 64.0, A.mult)
-            ts(r("BO"), r("IG"), cf(3), A.is_equal)
-            ts(r("XB"), r("IM"), cf(3), A.subtract, 15.0, A.is_equal)
-            ts(col("CB", 0), col("CB", 28), 0.5, A.mult, float(NV // 2 - LIM), A.add)
-            name("V", PRE_V)
-            iota(r("I16"), [[16, K]], 0)
-            iota(r("HR", RING, RING + K), [[0, K]], 1)
-            iota(r("CO", NV, NX), [[0, K]], WD)
-            iota(r("MO", NV, NX), [[0, K]], 0)
-            iota(r("Q", 0, 16), [[0, 16]], 0)
-            for m, nb in (("MCB", 72), ("MCA", 108)):
-                iota(r(m), [[0, 12 * nb]], 1)
-                op("G", lambda m=m, nb=nb: g.affine_select(T[m][:, :], T[m][:, :], [[0, 12], [1, nb]], A.is_gt, 0.0, 0, 0), r(m), [r(m)])
-                if m == "MCB":
-                    iota(r("W1", NV, WD), [[0, NG]], 0)
-                    iota(r("W1", WD, WY), [[0, K]], 1)
-            iota(r("I1"), [[1, K]], 1)
-            for u in (2, 3):
-                iota(r("W%d" % u, NV, WD), [[0, NG]], 0)
-                iota(r("W%d" % u, WD, WY), [[0, K]], 1)
-            for k in range(16):
-                dma("S", (T.MO[k:128:16, 0:NV], [("MO", 0, NV)], []), hbm(T.mo[:, :]), "lm", [(None, [("sentog0", 0, 1)], [])])
-            for u in (1, 2):
-                for i in range(4):
-                    dma("S", r("Z%d" % u, 440 * i, 440 * (i + 1)), r("ZC"), "z%d" % u)
-        else:
-            tl = "TLu"
-            scan(r("R", 0, NV), r(W, 0, NV), r(W, 0, NV), A.add, A.max)
-            ts(r("R", NV, NX), r("I1"), col("R", NV - 1), A.add)
-            compact(108, "MCA", "TLu", lambda bl: [r("BA", 0, 12)], lambda: None, CA)
-            copy(r("PTu"), ind("PR", NX, "TLu", 0, 12))
-            copy(r("P", 0, K), r("PTu"))
-            lists()
-        for d in range(1, 8):
-            mm(r("pa", (d - 1) * GH, d * GH), r(perm[(d - 1) % 3]), r("LG%d" % t, (d - 1) * GH, d * GH), True, True, inc=d == 7)
-        act(r("Y", NV, WD), r("pa", 0, NG), F.Copy)
-        for c in range(3):
-            act(r("V", CH * c, CH * (c + 1)), ind("Y", WY, "PTu", 48 * c, 48 * (c + 1)), F.Copy)
-        copy(r("V", 3 * CH, 4 * CH), ind("Y", WY, "PTu", 144, 192))
-        act(r("OLD"), ind("Y", WY, tl, 0, 12), F.Copy)
-        for c in (0, 3, 1, 2):
-            a, b = CH * c, CH * (c + 1)
-            scan(r("SB", a, b), r("M64"), r("V", a, b), A.add, A.min)
-            if c == 2:
-                ts(r("Qm"), r("SB", 15, 3072, 16), 0.0, A.is_lt, 64.0, A.mult)
-                mm(r("pa", 0, K), r("N1"), r("SB", 15, 3072, 16), True, False)
-                mm(r("pa", 0, K), r("N1"), r("Qm"), False, False)
-            scan(r("SA", a, b), r("M0"), r("V", a, b), A.mult, A.max)
-        mm(r("pa", 0, K), r("Id"), r("SA", 15, 3072, 16), False, True)
-        name("A", 2)
-        act(r("JK"), r("Qm"), F.Identity, bias=1.0, scale=-1.0 / 64, acc=col("CB", 16 + 4 * t))
-        act(r("EB"), r("ONE"), F.Relu, bias=col("CB", 4 * t), scale=col("CB", 16 + 4 * t))
-        if t + 1 < RO:
-            act(col("CB", 17 + 4 * t), col("CB", 16 + 4 * t), F.Identity, bias=col("CB", 4 * t))
-        tt(r("NEW"), r("OLD"), r("pa", 0, K), A.max)
-        copy(ind("Y", WY, tl, 0, 12), r("NEW"))
+    def candidates(t, gap, mid=None):
         st = (ST * t) % RING
         ts(r("HR", 0, RING - st), r("Y", S0 + st, S0 + RING), 0.0, A.is_ge)
         if st:
             ts(r("HR", RING - st, RING), r("Y", S0, S0 + st), 0.0, A.is_ge)
-        scan(r("R", 0, RING + K), r("HR"), r("HR"), A.add, A.max)
 
-        def rbase(bl, st=st):
+        def rbase(bl):
             ts(r("BA", 0, 12), bl, 16.0, A.mult, float(S0 + st), A.add)
             if st == 0:
                 ts(r("BB", 0, 12), bl, RING // 16 - 0.5, A.is_ge, float(TOP), A.mult)
@@ -338,99 +269,234 @@ def build(g, core, T, topo):
             ts(r("BB", 0, 12), bl, (RING - st) // 16 - 0.5, A.is_ge, -float(RING), A.mult)
             ts(r("BC", 0, 12), bl, RING // 16 - 0.5, A.is_ge, float(RING + TOP - st), A.mult)
             return [r("BA", 0, 12), r("BB", 0, 12), r("BC", 0, 12)]
-        compact(72, "MCB", "RLu", rbase, lambda: name("V", GAP[t]))
-        copy(r("PT2"), ind("PR", NX, "RLu", 0, 12))
-        for j in range(3):
-            mm(r("m%d" % j), r("N2"), r("Y", 512 * j, 512 * (j + 1)), True, False)
-        mm(r("pa", 0, NG), r("N7"), r("G%d" % t), True, False, inc=True)
-        name("A", 16)
-        dv = DV[t]
-        dm = (K - dv) // 4 * 2
-        for a, b in ((0, dm), (dm, K - dv)):
-            act(r("DG", 16 * a, 16 * b), ind("Y", WY, "PT2", a, b), F.Relu, scale=-1.0)
-        act(r("OL2"), ind("Y", WY, "RLu", 0, 12), F.Copy)
-        side = [lambda: copy(r("CTu"), ind("CO", NX, "RLu", 0, 12)), lambda: copy(r("OI"), ind("Y", WY, "RLu", 0, 12)),
-                lambda: ts(r("OI"), r("OI"), 1, A.bitwise_and), lambda: tt(r("OM"), ind("MO", NX, "RLu", 0, 12), r("OI"), A.mult)]
-        if t == RO - 1:
-            side += [lambda: ts(r("OY", 0, S0), r("Y", 0, S0), -1.0, A.max), lambda: ts(r("OY", NV - TOP, NV), r("Y", NV - TOP, NV), -1.0, A.max)]
-        late = side[EARLY[t]:]
-        side = side[:EARLY[t]]
-        for f in side[:-1]:
-            name("V", 1)
-            f()
-        name("V", 16)
-        if t:
-            ksum("pd", "DG", 0, dm)
-        for j in range(3):
-            mm(r("m%d" % j), r("Id"), r(W, 512 * j, 512 * (j + 1)), False, True)
-        side[-1]()
-        mm(r("pc", 0, NG), r("Id"), r(W, NV, WD), True, False)
-        for a in (0, NG // 2):
-            mm(r("pc", a, a + NG // 2), r("N2"), r("Y", WD, WD + NG // 2), False, a > 0)
-        if dv and DFIRST[t]:
-            ts(r("DG", 16 * (K - dv), 16 * K), ind("Y", WY, "PT2", K - dv, K), 0.0, A.is_lt)
-        for j in range(3):
-            tt(r(Wn, 512 * j, 512 * (j + 1)), r("m%d" % j), r(Z, 512 * j, 512 * (j + 1)), A.is_ge)
-        tt(r("NS%d" % t), r("pc", 0, NG), r(Z, NV, WD), A.is_ge)
-        send("NS%d" % t, "LN%d" % t, "an%d" % t, "on%d" % t)
-        if dv and not DFIRST[t]:
-            ts(r("DG", 16 * (K - dv), 16 * K), ind("Y", WY, "PT2", K - dv, K), 0.0, A.is_lt)
-        if t == 0:
-            ksum("pd", "DG", 0, dm)
-        ksum("pd", "DG", dm, K)
-        hw = WD + 16
-        for f in late:
-            f()
-        for i, (a, m, b) in enumerate(HV[t]):
-            if m > a:
-                copy(r("HG", 16 * a, 16 * m), ind(Wn, hw, "CTu", a, m))
-            if b > m:
-                act(r("HG", 16 * m, 16 * b), ind(Wn, hw, "CTu", m, b), F.Copy)
-            if i == len(HV[t]) - 1:
-                mm(r("pb", 0, K), r("BO"), r("Ff"), True, True)
-                mm(r("pd", 0, K), r("N4"), r("Ff"), True, False)
-                mm(r("pd", 0, K), r("N1"), r("OL2"), False, True)
-            ksum("ph", "HG", a, b)
-            if i == len(HV[t]) - 2:
-                tt(r("Ff"), r("OM"), r("pd", 0, K), A.min)
-        act(r("A1"), r("pd", 0, K), F.Identity, bias=-1.0)
-        act(r("AB"), r("pb", 0, K), F.Abs, bias=-8.0)
-        act(r("RWn"), r("AB"), F.Sign, bias=8.0, scale=-1.0)
-        if t == RO - 1:
-            for a, b, s1, s2 in ((0, S0, "s0", "s1"), (NV - TOP, NV, "s2", "s3")):
-                act(r("OF", a, b), r("Y", a, b), F.Relu, bias=-4.0, scale=-4.0)
-                dma("S", hbm(T.yy[:, a:b]), r("OY", a, b), s1)
-                dma("S", hbm(T.yf[:, a:b]), r("OF", a, b), s2)
-        ts(r("FR"), r("ph", 0, K), 0.5, A.is_lt)
-        scan(r("Q", 1, K + 1), r("FR"), r("EB"), A.add, A.min)
-        mm(r("pc", 0, K), r("Id"), r("Q", 1, K + 1), True, False)
-        mm(r("pc", 0, K), r("N1"), r("Q", 0, K), False, True)
-        tt(r("TA"), r("A1"), r("pc", 0, K), A.mult)
-        act(r("GO"), r("pc", 0, K), F.Copy)
-        tt(ind("Y", WY, "RLu", 0, 12), r("TA"), r("OL2"), A.add)
-        border(t + 1)
-        if t + 1 < RO:
-            send("G%d" % (t + 1), "LG%d" % (t + 1), "ag%d" % (t + 1), "og%d" % (t + 1))
-        tt(ind(Wn, WY, "RLu", 0, 12), r("GO"), r("RWn"), A.mult)
+        compact("HR", NBR, "MCB", "RWR", "RLu", rbase, gap, 0, mid)
+
+    def ksum(bank, src, a, b):
+        for k in range(16):
+            mm(r(bank, a, b), r("Id"), r(src, 16 * a + k, 16 * b, 16), k == 0, k == 15)
+
+    def facing(src, first):
         for d in range(1, 8):
-            mm(r("pa", (d - 1) * GH, d * GH), r(perm[(d - 1) % 3]), r("LN%d" % t, (d - 1) * GH, d * GH), False, False)
-        mm(r("pa", 0, NG), r("N7"), r("G%d" % (t + 1)), False, True)
-        act(r("NF"), r("pa", 0, NG), F.Sign, bias=-4.44)
-        if t + 1 < RO:
-            act(col("CB", 4 * t + 4), col("Q", K), F.Identity, bias=col("CB", 17 + 4 * t), scale=-1.0)
+            mm(r("pa", (d - 1) * GH, d * GH), r(perm[(d - 1) % 3]), r(src, (d - 1) * GH, d * GH), first, first or d == 7, inc=d == 7)
+
+    for t in range(RO):
+        W, Wn, YW = "W%d" % t, "W%d" % (t + 1), "Y%d" % t
+        last = t == RO - 1
+        todo = {"A": list(range(CFG["NA"][t])), "V": list(range(CFG["NA"][t], 16))}
+
+        def name(q, n, todo=todo, W=W, t=t):
+            for _ in range(n):
+                if todo[q]:
+                    k = todo[q].pop(0)
+                    if q == "A":
+                        silu(ind("Z", WY, "TU", 12 * k, 12 * k + 12), r("BIG", t * K, (t + 1) * K))
+                    else:
+                        copy(ind(W, WY, "TU", 12 * k, 12 * k + 12), r("ONE"))
+
+        def absent(a, b, YW=YW):
+            for j in range(a, b):
+                mm(r("m%d" % j), r(YW), r("Y", 512 * j, 512 * (j + 1)), True, False)
+
+        def wanted(ghosts, a, b, W=W):
+            if ghosts is None:
+                mm(r("pd", 0, NG), r("PW"), r(W, NV, WD), False, True)
+            for j in range(a, b):
+                mm(r("m%d" % j), r("PW"), r(W, 512 * j, 512 * (j + 1)), False, True)
+
+        if t == 0:
+            fill(r("W0", 0, NV - TOP), 0.0)
+            copy(r("G0"), ind("Y", NV, "BDu", 0, 14))
+            send("G0", "LG0", "ag0", "og0")
+            ts(r("W0", *top), r("Y", *top), 0.0, A.is_lt)
+            tt(r("X0"), r("PR", *top), r("PR", NV, NX), A.subtract)
+            act(r("JS"), r("Y", 0, NV), F.Sign, bias=0.5, acc=col("CB", 28))
+            ts(r("P1"), r("IM", 0, 128), cf(6), A.is_equal)
+            tt(r("X0"), r("X0"), r("W0", *top), A.mult)
+            ts(r("P2"), r("IM", 0, 128), cf(4), A.is_equal)
+            tt(r("P", 0, K), r("X0"), r("PR", NV, NX), A.add)
+            lists()
+            name("A", CFG["PRE"])
+            iota(r("MCB"), [[0, 12], [128, NBR]], 0)
+            iota(r("I16"), [[16, K]], 12)
+            const(r("W0", NV, WY), 0)
+            iota(r("OFF"), [[32, CS], [0, 16]], 32)
+            iota(r("M1"), [[0, CS], [-32, 16]], 20)
+            iota(r("M0"), [[0, CS], [32, 16]], 0)
+            fill(r("RWR", NBR, 80), 0.0)
+            copy(r("PTu"), r("P", 0, K))
+
+            def gap0():
+                for n in DIAG:
+                    if n != "Id":
+                        ts(r(n), r("Id"), DIAG[n], A.mult)
+                ts(r("BO"), r("IG"), cf(3), A.is_equal)
+                ts(col("CB", 0), col("CB", 28), 0.5, A.mult, float(NV // 2 - LIM), A.add)
+            candidates(0, gap0)
+            after = [(None, [("sentog0", 0, 1)], [])]
+            dma("S", r("PR", 0, S0), hbm(T.pr[:, 0:S0]), "lq", after)
+            dma("S", r("CO", *ring), hbm(T.co[:, ring[0]:ring[1]]), "lc")
+            for k in range(16):
+                dma("S", (T.MO[k:128:16, ring[0]:ring[1]], [("MO", ring[0], ring[1])], []), hbm(T.mo[:, ring[0]:ring[1]]), "lm")
+            const(r("W1", NV, WD), 0)
+            const(r("W1", WD, WY), 1)
+            const(r("CO", 0, S0), NV)
+            const(r("CO", NV - TOP, NX), WD)
+            const(r("MO", 0, S0), 0)
+            const(r("MO", NV - TOP, NX), 0)
+            const(r("Q", 0, 16), 0)
+            name("V", 16)
+            absent(0, 2)
         else:
-            ts(r("OY", S0, NV - TOP), r("Y", S0, NV - TOP), -1.0, A.max)
-            dma("S", hbm(T.yy[:, S0:NV - TOP]), r("OY", S0, NV - TOP), "s4")
-            act(r("OF", S0, NV - TOP), r("Y", S0, NV - TOP), F.Relu, bias=-4.0, scale=-4.0)
-            dma("A", hbm(T.yf[:, S0:NV - TOP]), r("OF", S0, NV - TOP), "s5")
+            compact(W, NBT, "MCA", "RWT", "TLu", tbase, lambda: None, CFG["CA"])
+            copy(r("PTu"), ind("PR", NX, "TLu", 0, 12))
+            copy(r("P", 0, K), r("PTu"))
+        facing("LG%d" % t, True)
+        act(r("Y", NV, WD), r("pa", 0, NG), F.Copy)
+        av = CFG["AV"][t]
+        if av:
+            act(r("VA"), ind("Y", WY, "PTu", 0, CS), F.Copy)
+        if t:
+            act(r("OLD"), ind("Y", WY, "TLu", 0, 12), F.Copy)
+            lists()
+            name("V", CFG["VE"][t])
+        name("A", 16)
+        for c in range(av, K // CS):
+            a, b = CS * c, CS * (c + 1)
+            tt(r("VF", 16 * a, 16 * b), ind("Y", WY, "PTu", a, b), r("OFF"), A.add)
+            if c > av:
+                scan(back("SBf", 8 * (a - CS), 8 * a, 1), back("VF", 16 * (a - CS), 16 * a, 2), back("VF", 16 * (a - CS), 16 * a - 1, 2), A.min, A.min, 4096.0)
+                mm(r("pb", a - CS, a), r("Id"), r("SBf", 8 * (a - CS), 8 * a, 8), True, False)
+                mm(r("pb", a - CS, a), r("N1"), r("OFF", 0, 16 * CS, 16), False, True)
+            elif av:
+                scan(r("SBa"), r("M1"), r("VA"), A.max, A.min)
+                mm(r("pb", 0, CS), r("Id"), r("SBa", 15, 16 * CS, 16), True, True)
+        if av:
+            scan(r("SAa"), r("M0"), r("VA"), A.min, A.max)
+        a = K
+        scan(back("SBf", 8 * (a - CS), 8 * a, 1), back("VF", 16 * (a - CS), 16 * a, 2), back("VF", 16 * (a - CS), 16 * a - 1, 2), A.min, A.min, 4096.0)
+        mm(r("pb", a - CS, a), r("Id"), r("SBf", 8 * (a - CS), 8 * a, 8), True, False)
+        mm(r("pb", a - CS, a), r("N1"), r("OFF", 0, 16 * CS, 16), False, True)
+        for c in range(av, K // CS):
+            a, b = CS * c, CS * (c + 1)
+            scan(r("SAf", 8 * a, 8 * b), r("VF", 16 * a, 16 * b, 2), r("VF", 16 * a + 1, 16 * b, 2), A.max, A.max)
+            if c == av:
+                ts(r("Qm"), r("pb", 0, K), 0.0, A.is_lt)
+                mm(r("pa", 0, K), r("N64"), r("Qm"), True, False)
+                if av:
+                    mm(r("pa", 0, CS), r("N1"), r("SBa", 15, 16 * CS, 16), False, False)
+                    mm(r("pa", 0, CS), r("Id"), r("SAa", 15, 16 * CS, 16), False, False)
+                mm(r("pa", av * CS, K), r("N1"), r("SBf", 8 * av * CS, 8 * K, 8), False, False)
+        mm(r("pa", av * CS, K), r("Id"), r("SAf", 8 * av * CS + 7, 8 * K, 8), False, True)
+        mm(r("pd", 0, NG), r(YW), r("Y", NV, WD), True, False)
+        if t == 0:
+            iota(r("MCA"), [[0, 12], [128, NBT]], 0)
+            iota(r("BIG", K, RO * K), [[ZMARK[2] - ZMARK[1], 2], [0, K]], ZMARK[1])
+            const(r("RWT", NBT, 112), 1 << 16)
+            wanted(None, 0, 2)
+            copy(r("PT2"), ind("PR", NX, "RLu", 0, 12))
+            tt(r("Y", *top), r("Y", *top), r("pa", 0, K), A.max)
+            absent(2, 3)
+            wanted(False, 2, 3)
+        else:
+            tt(r("NEW"), r("OLD"), r("pa", 0, K), A.max)
+            copy(ind("Y", WY, "TLu", 0, 12), r("NEW"))
+            candidates(t, lambda: name("V", 1), lambda: absent(0, 2))
+            absent(2, 3)
+            copy(r("PT2"), ind("PR", NX, "RLu", 0, 12))
+            name("V", 16)
+            wanted(None, 0, 3)
+        dg, hg = CFG["DG"][t], CFG["HG"][t]
+        act(r("OL2"), ind("Y", WY, "RLu", 0, 12), F.Copy)
+        for i in range(3):
+            act(r("DG", 16 * dg[i], 16 * dg[i + 1]), ind("Y", WY, "PT2", dg[i], dg[i + 1]), F.Relu, scale=-1.0)
+            if i == 0:
+                act(r("SG"), ind("Y", NV, "BDu", 0, 14), F.Sign, bias=0.5)
+        copy(r("CTu"), ind("CO", NX, "RLu", 0, 12))
+        if dg[3] < K:
+            ts(r("DG", 16 * dg[3], 16 * K), ind("Y", WY, "PT2", dg[3], K), 0.0, A.is_lt)
+        tt(r("NS%d" % t), r("pd", 0, NG), r("Z", NV, WD), A.is_ge)
+        send("NS%d" % t, "LN%d" % t, "an%d" % t, "on%d" % t)
+        if t == 0:
+            for u in (2, 3):
+                const(r("W%d" % u, NV, WD), 0)
+                const(r("W%d" % u, WD, WY), 1)
+            const(r("OW", NV, NX), 0)
+        for j in range(3):
+            tt(r(Wn, 512 * j, 512 * (j + 1)), r("m%d" % j), r("Z", 512 * j, 512 * (j + 1)), A.is_ge)
+        hw = WD + 16
+        ksum("pd", "DG", 0, dg[1])
+        mm(r("pa", 0, NG), r("NH"), r("SG"), True, False)
+        mm(r("pa", 0, NG), r("NE"), r("SG"), False, False)
+        tt(r("OI"), ind("MO", NX, "RLu", 0, 12), r("OL2"), A.mult)
+        copy(r("HG", 0, 16 * hg[1]), ind(Wn, hw, "CTu", 0, hg[1]))
+        ksum("pd", "DG", dg[1], dg[2])
+        ksum("ph", "HG", 0, hg[1])
+        ts(r("OM"), r("OI"), 1, A.bitwise_and)
+        copy(r("HG", 16 * hg[1], 16 * hg[2]), ind(Wn, hw, "CTu", hg[1], hg[2]))
+        ksum("pd", "DG", dg[2], K)
+        ksum("ph", "HG", hg[1], hg[2])
+        act(r("JK"), r("Qm"), F.Identity, bias=1.0, scale=-1.0, acc=col("CB", 16 + 4 * t))
+        if hg[3] < K:
+            act(r("HG", 16 * hg[3], 16 * K), ind(Wn, hw, "CTu", hg[3], K), F.Copy)
+        act(r("EB"), r("ONE"), F.Relu, bias=col("CB", 4 * t), scale=col("CB", 16 + 4 * t))
+        facing("LN%d" % t, False)
+        act(r("NF"), r("pa", 0, NG), F.Identity, bias=EPS / 2 - 0.5)
+        if CFG["FF"][t]:
+            tt(r("Ff"), r("OM"), r("pd", 0, K), A.min)
+        copy(r("HG", 16 * hg[2], 16 * hg[3]), ind(Wn, hw, "CTu", hg[2], hg[3]))
+        if not CFG["FF"][t]:
+            ksum("ph", "HG", hg[2], K)
+            tt(r("Ff"), r("OM"), r("pd", 0, K), A.min)
+        mm(r("pb", 0, K), r("BO"), r("Ff"), True, True)
+        if CFG["FF"][t]:
+            ksum("ph", "HG", hg[2], K)
+        mm(r("pd", 0, K), r("N1"), r("ONE"), True, False)
+        mm(r("pd", 0, K), r("N8"), r("Ff"), False, False)
+        mm(r("pd", 0, K), r("N1"), r("OL2"), False, True)
+        if CFG["FF"][t]:
+            act(r("AB"), r("pb", 0, K), F.Abs, bias=-8.0)
+            act(r("TH"), r("AB"), F.Identity, bias=EPS / 2 - 8.0)
+        act(r("FR"), r("ph", 0, K), F.Relu, bias=1.0, scale=-1.0)
+        if not CFG["FF"][t]:
+            act(r("AB"), r("pb", 0, K), F.Abs, bias=-8.0)
+            act(r("TH"), r("AB"), F.Identity, bias=EPS / 2 - 8.0)
+        if not last:
+            act(col("CB", 17 + 4 * t), col("CB", 16 + 4 * t), F.Identity, bias=col("CB", 4 * t))
+        if last:
+            for (a, b), s1, s2 in (((0, S0), "s0", "s1"), (top, "s2", "s3")):
+                ts(r("OY", a, b), r("Y", a, b), -1.0, A.max)
+                dma("S", hbm(T.yy[:, a:b]), r("OY", a, b), s1)
+                ts(r("OF", a, b), r("Y", a, b), -1.0625, A.is_lt)
+                dma("S", hbm(T.yf[:, a:b]), r("OF", a, b), s2)
         tt(r("NT"), ind(Wn, NV, "BDu", 0, 14), r("NF"), A.max)
         copy(ind(Wn, NV, "BDu", 0, 14), r("NT"))
-    dma("S", hbm(T.yw[:, :]), (T.W3[0:128:16, 0:NV], [("W3", 0, NV)], []), "s6")
+        scan(r("Q", 1, K + 1), r("FR"), r("EB"), A.add, A.min)
+        if last:
+            act(r("OW", 0, NV), r(Wn, 0, NV), F.Relu, bias=-0.003, scale=1.003)
+        scan(r("GO"), r("Q", 1, K + 1), r("Q", 0, K), A.max, A.subtract)
+        tt(r("RW2"), ind(Wn, WY, "RLu", 0, 12), r("TH"), A.is_gt)
+        scan(r("TA"), r("GO"), r("pd", 0, K), A.max, A.mult)
+        tt(ind("Y", WY, "RLu", 0, 12), r("TA"), r("OL2"), A.add)
+        if not last:
+            act(r("G%d" % (t + 1)), ind("Y", NV, "BDu", 0, 14), F.Copy)
+            send("G%d" % (t + 1), "LG%d" % (t + 1), "ag%d" % (t + 1), "og%d" % (t + 1))
+            tt(ind(Wn, WY, "RLu", 0, 12), r("GO"), r("RW2"), A.mult)
+            act(col("CB", 4 * t + 4), col("Q", K), F.Identity, bias=col("CB", 17 + 4 * t), scale=-1.0)
+        else:
+            ts(r("OY", *ring), r("Y", *ring), -1.0, A.max)
+            dma("S", hbm(T.yy[:, ring[0]:ring[1]]), r("OY", *ring), "s4")
+            ts(r("OF", *ring), r("Y", *ring), -1.0625, A.is_lt)
+            dma("A", hbm(T.yf[:, ring[0]:ring[1]]), r("OF", *ring), "s5")
+            tt(ind("OW", NX, "RLu", 0, 12), r("GO"), r("RW2"), A.mult)
+            dma("S", hbm(T.yw[:, :]), (T.OW[0:128:16, 0:NV], [("OW", 0, NV)], []), "s6")
     return ops, Q
 
 
 def emit(g, T, ops, Q):
     total = {}
+    for o, nxt in zip(ops, ops[1:]):
+        if o["q"] == "P" and nxt["q"] != "P":
+            o["inc"] = True
     for o in ops:
         if o["sem"] is None:
             s = "q" + o["q"]
@@ -455,7 +521,7 @@ def emit(g, T, ops, Q):
                     hit = True
                 else:
                     hit = (w or pw) and a < acc[2] and acc[1] < b
-                    if hit and p["q"] == q and p["sem"] is None and o["sem"] is None and (q == "P" or (w and not SAME_QUEUE_WAW)):
+                    if hit and p["q"] == q == "P":
                         hit = False
                     if hit and p["sem"] is not None and p["sem"] == o["sem"]:
                         hit = False

@@ -7,6 +7,7 @@ NG = 7 * GH
 WD = NV + NG
 WY = WD + K
 NX = NV + K
+PR0, CO0, MO0 = 0, NX - S0, 2 * (NX - S0)
 CS = 48
 NBT, NBR = NV // 16, (RING + K) // 16
 B16, F16, F32, I32, U16 = "bfloat16", "float16", "float32", "int32", "uint16"
@@ -19,49 +20,51 @@ def sb(n, d):
 
 
 SCRATCH = {
-    "Y": sb(WY, B16), "PR": sb(NX, I32), "CO": sb(NX, I32), "MO": sb(NX, I32), "BD": sb(16, I32), "BDu": sb(16, U16),
-    "Z": sb(WY, F32), "ZC": sb(WY // 4, F32), "JS": sb(NV, B16),
-    "VA": sb(16 * CS, B16), "SAa": sb(16 * CS, B16), "SBa": sb(16 * CS, B16), "M0": sb(16 * CS, B16), "M1": sb(16 * CS, B16),
-    "VF": sb(16 * K, F16), "SAf": sb(8 * K, F16), "SBf": sb(16 + 8 * K, F16), "OFF": sb(16 * CS, B16),
-    "DG": sb(16 * K, B16), "HG": sb(16 * K, B16),
+    "Y": sb(WY, B16), "TAB": sb(MO0 + NX, I32), "BD": sb(16, I32), "BDu": sb(16, U16),
+    "Z": sb(WY, F32), "ZC": sb(WY // 4, F32), "RR": sb(NX // 2, F16), "ZB": sb(S0, B16), "H0": sb(K, B16),
+    "VA": sb(48 * CS, B16), "SAa": sb(48 * CS, B16), "SBa": sb(48 * CS, B16), "M0": sb(16 * CS, B16), "M1": sb(16 * CS, B16),
+    "VF": sb(16 * K, F16), "SAf": sb(8 * K, F16), "SBf": sb(8 * K, F16), "OFF": sb(16 * CS, B16),
+    "DG": sb(16 * K, B16), "HG": sb(16 * K, B16), "ON5": sb(512, B16), "T1": sb(12 * NBR, B16), "B1": sb(12 * NBR, B16),
     "MCA": sb(12 * NBT, B16), "MCB": sb(12 * NBR, B16), "FC": sb(12 * NBT, B16), "FS": sb(12 * NBT, B16),
-    "R": sb(NV // 2, B16), "HR": sb(RING + K, B16), "RWT": sb(112, F32), "RWR": sb(80, F32),
+    "R": sb(NV // 2, B16), "HR": sb(NX, B16), "RWT": sb(112, F32), "RWR": sb(80, F32),
     "F2": sb(K, B16), "Bu": sb(16, U16), "BA": sb(16, B16), "BB": sb(16, B16), "BC": sb(16, B16), "BF": sb(16, B16),
     "TLu": sb(16, U16), "RLu": sb(16, U16), "SEL": sb(16, U16),
-    "PTu": sb(K, U16), "PT2": sb(K, U16), "CTu": sb(K, U16), "TU": sb(K, U16), "P": sb(208, F32), "TT": sb(384, F32),
+    "PTu": sb(K, U16), "PT2": sb(K, U16), "CTu": sb(K, U16), "TU": sb(K, U16), "P": sb(K + 32, F32), "TT": sb(2 * K + 32, F32),
     "OLD": sb(K, B16), "OL2": sb(K, B16), "Qm": sb(K, B16), "NEW": sb(K, B16), "OI": sb(K, I32), "OM": sb(K, I32),
-    "Ff": sb(K, B16), "A1": sb(K, B16), "AB": sb(K, B16), "TH": sb(K, B16), "RW2": sb(K, B16), "FR": sb(K, B16),
+    "Ff": sb(K, B16), "AB": sb(K, B16), "TH": sb(K, B16), "RW2": sb(K, B16), "FR": sb(K, B16),
     "Q": sb(208, B16), "GO": sb(K, B16), "TA": sb(K, B16), "EB": sb(K, B16), "JK": sb(K, B16), "JL": sb(K, B16),
-    "SG": sb(NG, B16), "NF": sb(NG, B16), "NT": sb(NG, B16),
+    "SG": sb(NG, B16), "NF": sb(NG, B16), "WB": sb(NG, B16),
     "ONE": sb(K, B16), "BIG": sb(RO * K, F32), "I16": sb(K, F32), "X0": sb(K, F32),
-    "IP": sb(4, I32), "IM": sb(144, F32), "IG": sb(128, F32), "J": sb(12, F32), "SL": sb(12, F32), "CI": sb(64, I32), "CF": sb(96, F32),
+    "IP": sb(4, I32), "IM": sb(144, F32), "J": sb(12, F32), "SL": sb(12, F32), "CI": sb(64, I32), "CF": sb(128, F32),
     "SH": sb(12, F32), "BS": sb(12, F32), "CB": sb(32, F32),
     "XB": sb(144, B16), "XN": sb(144, B16), "X2": sb(144, B16), "OY": sb(NV, B16), "OF": sb(NV, B16), "OW": sb(NX, B16),
 }
-DIAG = {"Id": 1.0, "N1": -1.0, "N8": -0.125, "N64": -64.0, "NH": -0.5, "NE": EPS / 2, "PW": WW, "Y0": -WYS[0], "Y1": -WYS[1], "Y2": -WYS[2]}
-for _n in list(DIAG) + ["P1", "P2", "BO"]:
+DIAG = {"Id": 1.0, "N1": -1.0, "N8": -0.125, "N64": -64.0, "NH": -0.5, "NE": EPS / 2, "PW": WW, "Y0": -WYS[0], "Y1": -WYS[1], "Y2": -WYS[2],
+        "P4K": 4096.0, "N4K": -4096.0}
+for _n in list(DIAG) + ["P1", "P2", "BO", "DSH"]:
     SCRATCH[_n] = sb(128, B16)
 for _t in range(RO + 1):
     SCRATCH["W%d" % _t] = sb(WY, B16)
 for _t in range(RO):
     for _n in ("G", "NS", "LG", "LN"):
         SCRATCH["%s%d" % (_n, _t)] = sb(NG, B16)
-BANKS = ["m0", "m1", "m2", "pa", "pb", "pc", "pd", "ph"]
-for _n in BANKS:
-    SCRATCH[_n] = ("psum", [128, 512], F32)
+BANKS = {"m0": ("pm", 0), "m1": ("pm", 512), "m2": ("pm", 1024), "pc": ("px", 0), "ph": ("px", 512), "pa": ("pa", 0), "pb": ("pb", 0), "pd": ("pd", 0)}
+for _n, _w in (("pm", 1536), ("px", 1024), ("pa", 512), ("pb", 512), ("pd", 512)):
+    SCRATCH[_n] = ("psum", [128, _w], F32)
 
 SEMAPHORES = (["qV", "qA", "qP", "qG", "ly", "lb", "lt", "lp", "lq", "lc", "lm", "s0", "s1", "s2", "s3", "s4", "s5", "s6"]
               + ["%s%d" % (n, t) for n in ("ag", "an", "og", "on") for t in range(RO)])
 
 CFG = {
-    "NA": (14, 13, 13),
-    "AV": (1, 1, 1),
-    "PRE": 8,
-    "VE": (0, 1, 1),
-    "CA": 4,
-    "DG": ((0, 64, 128, 192),) * 3,
-    "HG": ((0, 64, 128, 172),) * 3,
-    "FF": (0, 0, 0),
+    "NA": (13, 10, 10),
+    "AV": (1, 3, 3),
+    "PRE": 7,
+    "TUF": 0, "AQ": 1, "JP": (1, 1, 1),
+    "VW": {"first": 0, "early": 0, "early2": 0, "new": 12, "put": 4, "ring": 8, "count": 4, "block": 20, "place": 12, "list": 12, "cand": 0},
+    "CA": 5,
+    "DG": (0, 64, 128, 192),
+    "HG": ((0, 64, 128, 152, 172), (0, 64, 128, 144, 156), (0, 64, 128, 144, 156)),
+    "RWV": 0, "PG": 2, "TO": 0, "SGE": 1, "LEAD": 3,
 }
 
 
@@ -70,18 +73,30 @@ def build(g, core, T, topo):
     ops = []
     Q = {"V": g.vector, "A": g.scalar, "P": g.tensor, "G": g, "S": g.sync}
 
+    def touched(name, a, b):
+        if name in ("pm", "px"):
+            return [(n, 0, 512) for n in BANKS if BANKS[n][0] == name and BANKS[n][1] < b and a < BANKS[n][1] + 512]
+        return [(name, a, b)]
+
     def r(name, a=None, b=None, s=None):
-        t = T[name]
         a = 0 if a is None else a
+        if name in BANKS:
+            t, o = T[BANKS[name][0]], BANKS[name][1]
+            b = 512 if b is None else b
+            return (t[:, o + a:o + b:s or 1], [(name, a, b)], [])
+        t = T[name]
         b = t.shape[1] if b is None else b
-        return (t[:, a:b] if s is None else t[:, a:b:s], [(name, a, b)], [])
+        return (t[:, a:b] if s is None else t[:, a:b:s], touched(name, a, b), [])
 
     def back(name, a, b, s):
         t = T[name]
-        return (t[:, b - 1::-s] if a == 0 else t[:, b - 1:a - 1:-s], [(name, a, b)], [])
+        return (t[:, b - 1::-s] if a == 0 else t[:, b - 1:a - 1:-s], touched(name, a, b), [])
 
     def ind(name, b, off, c, d):
         return (T[name][:, 0:b].indirect(T[off][:, c:d]), [(name, 0, b)], [(off, c, d)])
+
+    def table(a, off):
+        return (T.TAB[:, a:a + NX].indirect(T[off][:, 0:12]), [("TAB", a, a + NX)], [(off, 0, 12)])
 
     def op(q, fn, out, ins, sem=None, inc=True, cnt=16):
         rd = []
@@ -140,6 +155,12 @@ def build(g, core, T, topo):
     def const(o, c):
         iota(o, [[0, o[1][0][2] - o[1][0][1]]], c)
 
+    def select(o, i, pat, f, c, base, cm=1):
+        op("G", lambda: g.affine_select(o[0], i[0], pat, f, c, base, cm), o, [i])
+
+    def diag(n):
+        select(r(n), r("ZB", 0, 128), [[-1, 128]], A.not_equal, DIAG[n], 0)
+
     def dma(q, o, i, sem, extra=()):
         op(q, lambda: Q[q].dma_start(o[0], i[0]), o, [i] + list(extra), sem=sem)
 
@@ -168,65 +189,57 @@ def build(g, core, T, topo):
 
     dma("S", r("Y", 0, NV), hbm(T.y0[:, :]), "ly")
     dma("A", r("BD", 0, 14), hbm(T.bd[:, :]), "lb")
-    dma("A", r("PR", *top), hbm(T.pr[:, top[0]:top[1]]), "lt")
-    dma("S", r("PR", *ring), hbm(T.pr[:, ring[0]:ring[1]]), "lp", [r("Y", 0, NV)])
+    dma("A", r("TAB", *top), hbm(T.pr[:, top[0]:top[1]]), "lt")
     iota(col("IP", 0), [[0, 1]], 0, 1)
     iota(r("J"), [[16, 12]], 0)
     iota(r("IM"), [[1, 144]], 0)
-    iota(r("PR", NV, NX), [[1, K]], WD)
-    iota(r("IG"), [[16, 8], [0, 16]], 0)
-    const(r("BIG", 0, K), ZMARK[0])
-    const(r("HR", RING, RING + K), 1)
+    iota(r("TAB", NV, NX), [[1, K]], WD)
+    const(r("P", 0, 16), 0)
+    const(r("P", K + 16, K + 32), 0)
+    const(r("Z", WY // 4 * 3, WY), int(ZNONE))
     fill(r("ZC"), ZNONE)
-    for i in range(4):
+    for i in range(3):
         silu(r("Z", WY // 4 * i, WY // 4 * (i + 1)), r("ZC"))
-    fill(r("ONE"), 1.0)
+    fill(r("ZB"), 0.0)
+    for a, b in ((0, 336), (336, 672), (672, 1008), (1008, NV - TOP), (NV, NV + 208), (NV + 208, WY)):
+        dma("S", r("W0", a, b), r("ZB", 0, b - a), "lp", [r("Y", 0, NV)])
     ci = lambda j, n=1: r("CI", 4 * j, 4 * j + n)
     cf = lambda j, n=1: r("CF", 4 * j, 4 * j + n)
     ts(ci(0), col("IP", 0), 15, A.bitwise_and)
     ts(ci(1), col("IP", 0), 16, A.bitwise_and)
-    ts(ci(2), col("IP", 0), 4, A.arith_shift_right)
     copy(cf(0), col("IP", 0))
     copy(cf(1), ci(0))
     copy(cf(2), ci(1))
-    ts(ci(3), ci(2), -1.0, A.mult, 8.0, A.add)
     ts(r("SL"), r("J"), cf(1), A.add)
-    ts(ci(4), ci(3), 7, A.bitwise_and)
     ts(cf(3), cf(0), cf(1), A.subtract)
-    fill(r("Y", WD, WY), -1.0)
+    ts(cf(7), cf(2), -2.0, A.mult, 32.0, A.add)
     ts(cf(8, 12), r("SL"), 1.0 / 12, A.mult, 0.5 / 12 - 0.5, A.add)
-    ts(cf(16, 12), r("SL"), 32.0, A.mult, cf(2), A.add)
-    ts(r("Id"), r("IM", 0, 128), cf(0), A.is_equal)
-    copy(ci(8, 12), cf(8, 12))
-    ts(cf(4), ci(4), 16.0, A.mult, cf(1), A.add)
-    ts(cf(5), cf(3), -1.0, A.mult, 112.0, A.add)
-    ts(cf(12, 12), ci(8, 12), -383.0, A.mult)
     ts(r("XB"), r("IM"), cf(3), A.subtract, 15.0, A.is_equal)
-    ts(cf(6), cf(5), cf(1), A.add)
-    tt(cf(20, 12), cf(12, 12), cf(16, 12), A.add)
-    ts(r("SH"), r("SL"), 0.75, A.add)
-    copy(r("BDu", 0, 14), r("BD", 0, 14))
+    ts(cf(16, 12), r("SL"), 32.0, A.mult, cf(2), A.add)
+    copy(ci(8, 12), cf(8, 12))
     ts(r("XN"), r("XB"), -1.0, A.mult)
-    copy(r("SEL", 0, 12), cf(20, 12))
-    fill(r("X2", 143, 144), 0.0)
-    tt(r("X2", 0, 143), r("XB", 0, 143), r("XB", 1, 144), A.add)
+    ts(r("SH"), r("SL"), 0.75, A.add)
+    ts(cf(24, 12), ci(8, 12), 12.0, A.mult, 5.5, A.add)
+    ts(cf(12, 12), ci(8, 12), -383.0, A.mult)
+    scan(r("X2", 0, 143), r("XB", 0, 143), r("XB", 1, 144), A.min, A.add, 1.0)
+    tt(cf(28, 12), r("SL"), cf(24, 12), A.is_ge)
+    tt(cf(20, 12), cf(12, 12), cf(16, 12), A.add)
+    copy(r("BDu", 0, 14), r("BD", 0, 14))
+    ts(cf(24, 12), cf(28, 12), cf(7), A.mult)
 
-    def lists():
-        copy(r("P", K, K + 16), r("P", 0, 16))
-        tr(r("TT", 0, K), r("P", 0, K))
-        tr(r("TT", K, 2 * K), r("P", 16, K + 16))
-        copy(r("TU"), ind("TT", 2 * K, "SEL", 0, 12))
-
-    def compact(row, nb, mask, rw, out, bases, gap, na=0, mid=None):
-        nv = 12 - na
+    def counted(row, run, nb, n):
         for j in range(8):
             mm(r("pb", 0, nb), r("XN", 15 - 2 * j, 143 - 2 * j), r(row, 2 * j + 1, 16 * nb, 16), j == 0, False)
-        scan(r("R", 0, 8 * nb), r(row, 0, 16 * nb, 2), r(row, 1, 16 * nb, 2), A.add, A.add)
-        ends = r("R", 7, 8 * nb, 8)
+        scan(r(run, 0, n // 2), r(row, 0, n, 2), r(row, 1, n, 2), A.add, A.add)
+
+    def spread(run, nb):
         for j in range(8):
-            mm(r("pb", 0, nb), r("X2", 14 - 2 * j, 142 - 2 * j), r("R", j, 8 * nb, 8), False, j == 7)
-        if mid:
-            mid()
+            mm(r("pb", 0, nb), r("X2", 14 - 2 * j, 142 - 2 * j), r(run, j, 8 * nb, 8), False, j == 7)
+
+    def blocks(run, nb, mask, rw, na):
+        nv = 12 - na
+        ends = r(run, 7, 8 * nb, 8)
+        spread(run, nb)
         for b in range(nv, 12):
             act(r("JK" if b % 2 else "JL", 0, nb), ends, F.Sign, bias=col("SH", b), scale=-1.0, acc=col("BS", b))
         for b in range(nv):
@@ -235,41 +248,33 @@ def build(g, core, T, topo):
             act(r(rw, 0, nb), r("pb", 0, nb), F.Copy)
         else:
             copy(r(rw, 0, nb), r("pb", 0, nb))
-        scan(r("FS", 0, nv * nb), r(mask, 0, nv * nb), r("FC", 0, nv * nb), A.min, A.add)
-        bl = r("FS", nb - 1, nv * nb, nb)
-        if na:
+        if mask:
+            scan(r("FS", 0, nv * nb), r(mask, 0, nv * nb), r("FC", 0, nv * nb), A.min, A.add)
             ts(r("Bu", nv, 12), r("BS", nv, 12), 0.5, A.mult, nb / 2, A.add)
+            bl = r("FS", nb - 1, nv * nb, nb)
+        else:
+            h = nb // 2
+            scan(r("SAf", 16, 16 + 12 * h), r("FC", 0, 12 * nb, 2), r("FC", 1, 12 * nb, 2), A.add, A.add)
+            ts(r("W0", *top), r("Y", *top), 0.0, A.is_lt)
+            ts(col("CB", 0), col("RR", NX // 2 - 1), -float(K + LIM), A.add)
+            bl = r("BF", 0, 12)
+            tt(bl, r("SAf", 15 + h, 16 + 12 * h, h), r("SAf", 15, 16 + 11 * h, h), A.subtract)
+            copy(r("PTu"), r("P", 16, K + 16))
         copy(r("Bu", 0, nv), bl)
-        tt(r("F2"), ind(rw, SCRATCH[rw][1][1], "Bu", 0, 12), r("I16"), A.is_le)
-        bs = bases(bl)
+        return bl
+
+    def inside(first, rest):
+        for i, x in enumerate(first):
+            mm(r("pc", 0, 12), r("Id"), x, i == 0, False)
         for a in range(16):
-            mm(r("pc", 0, 12), r("XB", 15 - a, 143 - a), r("F2", a, K, 16), a == 0, False)
-        for i in range(len(bs)):
-            mm(r("pc", 0, 12), r("Id"), bs[i], False, i == len(bs) - 1)
-        gap()
-        copy(r(out, 0, 12), r("pc", 0, 12))
+            mm(r("pc", 0, 12), r("XB", 15 - a, 143 - a), r("F2", a, K, 16), a == 0 and not first, False)
+        for i, x in enumerate(rest):
+            mm(r("pc", 0, 12), r("Id"), x, False, i == len(rest) - 1)
 
-    def tbase(bl):
-        ts(r("BA", 0, 12), r("Bu", 0, 12), 16.0, A.mult)
-        ts(r("BF", 0, 12), r("Bu", 0, 12), NBT - 0.5, A.is_ge)
-        tt(r("BB", 0, 12), r("BF", 0, 12), r("SL"), A.mult)
-        return [r("BA", 0, 12), r("BB", 0, 12)]
-
-    def candidates(t, gap, mid=None):
-        st = (ST * t) % RING
-        ts(r("HR", 0, RING - st), r("Y", S0 + st, S0 + RING), 0.0, A.is_ge)
-        if st:
-            ts(r("HR", RING - st, RING), r("Y", S0, S0 + st), 0.0, A.is_ge)
-
-        def rbase(bl):
-            ts(r("BA", 0, 12), bl, 16.0, A.mult, float(S0 + st), A.add)
-            if st == 0:
-                ts(r("BB", 0, 12), bl, RING // 16 - 0.5, A.is_ge, float(TOP), A.mult)
-                return [r("BA", 0, 12), r("BB", 0, 12)]
-            ts(r("BB", 0, 12), bl, (RING - st) // 16 - 0.5, A.is_ge, -float(RING), A.mult)
-            ts(r("BC", 0, 12), bl, RING // 16 - 0.5, A.is_ge, float(RING + TOP - st), A.mult)
-            return [r("BA", 0, 12), r("BB", 0, 12), r("BC", 0, 12)]
-        compact("HR", NBR, "MCB", "RWR", "RLu", rbase, gap, 0, mid)
+    def places():
+        for a, b in ((0, 512), (512, 12 * NBR)):
+            mm(r("px", a, b), r("P4K"), r("T1", a, b), True, False)
+            mm(r("px", a, b), r("DSH"), r("ON5", 0, b - a), False, False)
 
     def ksum(bank, src, a, b):
         for k in range(16):
@@ -282,211 +287,363 @@ def build(g, core, T, topo):
     for t in range(RO):
         W, Wn, YW = "W%d" % t, "W%d" % (t + 1), "Y%d" % t
         last = t == RO - 1
-        todo = {"A": list(range(CFG["NA"][t])), "V": list(range(CFG["NA"][t], 16))}
+        na, av = CFG["NA"][t], CFG["AV"][t]
+        at = {"A": 0, "V": 12 * na}
 
-        def name(q, n, todo=todo, W=W, t=t):
+        def name_a(n=1, at=at, na=na, t=t):
             for _ in range(n):
-                if todo[q]:
-                    k = todo[q].pop(0)
-                    if q == "A":
-                        silu(ind("Z", WY, "TU", 12 * k, 12 * k + 12), r("BIG", t * K, (t + 1) * K))
-                    else:
-                        copy(ind(W, WY, "TU", 12 * k, 12 * k + 12), r("ONE"))
+                if at["A"] < 12 * na:
+                    silu(ind("Z", WY, "TU", at["A"], at["A"] + 12), r("BIG", t * K, (t + 1) * K))
+                    at["A"] += 12
+
+        def name_v(n, at=at, W=W):
+            while n > 0 and at["V"] < K:
+                c = at["V"]
+                d = min(c + n, c // 12 * 12 + 12)
+                copy(ind(W, WY, "TU", c, d), r("ONE", 0, 16 * (d - c)))
+                at["V"], n = d, n - (d - c)
+
+        def wait(where, t=t):
+            if t:
+                name_v(CFG["VW"][where])
 
         def absent(a, b, YW=YW):
             for j in range(a, b):
                 mm(r("m%d" % j), r(YW), r("Y", 512 * j, 512 * (j + 1)), True, False)
 
-        def wanted(ghosts, a, b, W=W):
-            if ghosts is None:
-                mm(r("pd", 0, NG), r("PW"), r(W, NV, WD), False, True)
-            for j in range(a, b):
+        def wanted(b, W=W):
+            mm(r("pd", 0, NG), r("PW"), r(W, NV, WD), False, True)
+            for j in range(b):
                 mm(r("m%d" % j), r("PW"), r(W, 512 * j, 512 * (j + 1)), False, True)
 
+        def turn():
+            tr(r("TT", 0, K), r("P", 16, K + 16))
+            tr(r("TT", K, 2 * K + 32), r("P"))
+
+        def lists():
+            copy(r("TU"), ind("TT", 2 * K + 32, "SEL", 0, 12))
+
         if t == 0:
-            fill(r("W0", 0, NV - TOP), 0.0)
+            ts(r("H0"), r("Y", *top), 0.0, A.is_ge, 4096.0, A.mult)
             copy(r("G0"), ind("Y", NV, "BDu", 0, 14))
             send("G0", "LG0", "ag0", "og0")
-            ts(r("W0", *top), r("Y", *top), 0.0, A.is_lt)
-            tt(r("X0"), r("PR", *top), r("PR", NV, NX), A.subtract)
-            act(r("JS"), r("Y", 0, NV), F.Sign, bias=0.5, acc=col("CB", 28))
-            ts(r("P1"), r("IM", 0, 128), cf(6), A.is_equal)
-            tt(r("X0"), r("X0"), r("W0", *top), A.mult)
-            ts(r("P2"), r("IM", 0, 128), cf(4), A.is_equal)
-            tt(r("P", 0, K), r("X0"), r("PR", NV, NX), A.add)
+            tt(r("X0"), r("TAB", *top), r("H0"), A.add)
+            tt(cf(28, 12), cf(24, 12), cf(20, 12), A.add)
+            ts(r("HR", RING + K, RING + K + S0), r("Y", 0, S0), 0.0, A.is_ge)
+            const(r("BIG", 0, K), ZMARK[0])
+            tt(r("P", 16, K + 16), r("X0"), r("TAB", NV, NX), A.min)
+            copy(r("SEL", 0, 12), cf(28, 12))
+            ts(r("HR", RING + K + S0, NX), r("Y", *top), 0.0, A.is_ge)
+            turn()
+            ts(r("HR", 0, RING), r("Y", *ring), 0.0, A.is_ge)
             lists()
-            name("A", CFG["PRE"])
-            iota(r("MCB"), [[0, 12], [128, NBR]], 0)
+            name_a(CFG["PRE"])
+            const(r("HR", RING, RING + K), 1)
             iota(r("I16"), [[16, K]], 12)
-            const(r("W0", NV, WY), 0)
+            const(r("RWR", NBR, 80), 0)
+            diag("Id")
+            const(r("ONE"), 1)
+            select(r("P1"), r("ZB", 0, 128), [[16, 8], [-1, 16]], A.not_equal, 1.0, -112)
+            select(r("P2", 0, 16), r("ZB", 0, 16), [[-1, 16]], A.not_equal, 1.0, 0)
+            select(r("P2", 16, 128), r("ZB", 0, 112), [[16, 7], [-1, 16]], A.not_equal, 1.0, -112)
+            const(r("Y", WD, WY), -1)
             iota(r("OFF"), [[32, CS], [0, 16]], 32)
+            diag("N1")
+            diag("Y0")
+            diag("PW")
             iota(r("M1"), [[0, CS], [-32, 16]], 20)
             iota(r("M0"), [[0, CS], [32, 16]], 0)
-            fill(r("RWR", NBR, 80), 0.0)
-            copy(r("PTu"), r("P", 0, K))
-
-            def gap0():
-                for n in DIAG:
-                    if n != "Id":
-                        ts(r(n), r("Id"), DIAG[n], A.mult)
-                ts(r("BO"), r("IG"), cf(3), A.is_equal)
-                ts(col("CB", 0), col("CB", 28), 0.5, A.mult, float(NV // 2 - LIM), A.add)
-            candidates(0, gap0)
+            diag("N64")
+            counted("HR", "RR", NBR, NX)
+            copy(r("SAf", 0, 16), r("ZB", 0, 16))
+            bl = blocks("RR", NBR, None, "RWR", 0)
+            ts(r("BA", 0, 12), bl, 16.0, A.mult, float(S0), A.add)
+            ts(r("BB", 0, 12), bl, RING // 16 - 0.5, A.is_ge, float(TOP), A.mult)
+            tt(r("F2"), ind("RWR", 80, "Bu", 0, 12), r("I16"), A.is_le)
+            inside([], [r("BA", 0, 12), r("BB", 0, 12)])
+            name_v(12)
+            copy(r("RLu", 0, 12), r("pc", 0, 12))
             after = [(None, [("sentog0", 0, 1)], [])]
-            dma("S", r("PR", 0, S0), hbm(T.pr[:, 0:S0]), "lq", after)
-            dma("S", r("CO", *ring), hbm(T.co[:, ring[0]:ring[1]]), "lc")
+            dma("S", r("TAB", PR0, PR0 + NV - TOP), hbm(T.pr[:, 0:NV - TOP]), "lq", after)
+            dma("S", r("TAB", CO0 + ring[0], CO0 + ring[1]), hbm(T.co[:, ring[0]:ring[1]]), "lc")
             for k in range(16):
-                dma("S", (T.MO[k:128:16, ring[0]:ring[1]], [("MO", ring[0], ring[1])], []), hbm(T.mo[:, ring[0]:ring[1]]), "lm")
+                a, b = MO0 + ring[0], MO0 + ring[1]
+                dma("S", (T.TAB[k:128:16, a:b], [("TAB", a, b)], []), hbm(T.mo[:, ring[0]:ring[1]]), "lm")
+            for (a, b), s in (((0, S0), "s2"), (top, "s3")):
+                dma("S", hbm(T.yf[:, a:b]), r("ZB", 0, b - a), s)
+            const(r("TAB", CO0 + NV - TOP, CO0 + NX), WD)
             const(r("W1", NV, WD), 0)
             const(r("W1", WD, WY), 1)
-            const(r("CO", 0, S0), NV)
-            const(r("CO", NV - TOP, NX), WD)
-            const(r("MO", 0, S0), 0)
-            const(r("MO", NV - TOP, NX), 0)
-            const(r("Q", 0, 16), 0)
-            name("V", 16)
-            absent(0, 2)
+            name_v(K)
         else:
-            compact(W, NBT, "MCA", "RWT", "TLu", tbase, lambda: None, CFG["CA"])
-            copy(r("PTu"), ind("PR", NX, "TLu", 0, 12))
-            copy(r("P", 0, K), r("PTu"))
+            blocks("R", NBT, "MCA", "RWT", CFG["CA"])
+            tt(r("F2"), ind("RWT", 112, "Bu", 0, 12), r("I16"), A.is_le)
+            ts(r("BF", 0, 12), r("Bu", 0, 12), NBT - 0.5, A.is_ge)
+            ts(r("BA", 0, 12), r("Bu", 0, 12), 16.0, A.mult)
+            tt(r("BB", 0, 12), r("BF", 0, 12), r("SL"), A.mult)
+            inside([], [r("BA", 0, 12), r("BB", 0, 12)])
+            copy(r("TLu", 0, 12), r("pc", 0, 12))
+            if t == 1:
+                act(col("CB", 31), col("SH", 0), F.Copy, scale=4096.0)
+                act(r("DSH"), r("Id"), F.Copy, scale=col("CB", 31))
+            if CFG["PG"] == 2:
+                copy(r("P", 16, K + 16), table(PR0, "TLu"))
+            copy(r("PTu"), table(PR0, "TLu"))
+            if CFG["PG"] == 1:
+                copy(r("P", 16, K + 16), table(PR0, "TLu"))
+            if CFG["PG"] == 0:
+                copy(r("P", 16, K + 16), r("PTu"))
+            turn()
+            if CFG["TUF"] == 2:
+                lists()
+                name_a(CFG["AQ"])
+                wait("first")
         facing("LG%d" % t, True)
-        act(r("Y", NV, WD), r("pa", 0, NG), F.Copy)
-        av = CFG["AV"][t]
-        if av:
-            act(r("VA"), ind("Y", WY, "PTu", 0, CS), F.Copy)
         if t:
-            act(r("OLD"), ind("Y", WY, "TLu", 0, 12), F.Copy)
-            lists()
-            name("V", CFG["VE"][t])
-        name("A", 16)
-        for c in range(av, K // CS):
-            a, b = CS * c, CS * (c + 1)
-            tt(r("VF", 16 * a, 16 * b), ind("Y", WY, "PTu", a, b), r("OFF"), A.add)
-            if c > av:
-                scan(back("SBf", 8 * (a - CS), 8 * a, 1), back("VF", 16 * (a - CS), 16 * a, 2), back("VF", 16 * (a - CS), 16 * a - 1, 2), A.min, A.min, 4096.0)
-                mm(r("pb", a - CS, a), r("Id"), r("SBf", 8 * (a - CS), 8 * a, 8), True, False)
-                mm(r("pb", a - CS, a), r("N1"), r("OFF", 0, 16 * CS, 16), False, True)
-            elif av:
-                scan(r("SBa"), r("M1"), r("VA"), A.max, A.min)
-                mm(r("pb", 0, CS), r("Id"), r("SBa", 15, 16 * CS, 16), True, True)
-        if av:
-            scan(r("SAa"), r("M0"), r("VA"), A.min, A.max)
-        a = K
-        scan(back("SBf", 8 * (a - CS), 8 * a, 1), back("VF", 16 * (a - CS), 16 * a, 2), back("VF", 16 * (a - CS), 16 * a - 1, 2), A.min, A.min, 4096.0)
-        mm(r("pb", a - CS, a), r("Id"), r("SBf", 8 * (a - CS), 8 * a, 8), True, False)
-        mm(r("pb", a - CS, a), r("N1"), r("OFF", 0, 16 * CS, 16), False, True)
-        for c in range(av, K // CS):
-            a, b = CS * c, CS * (c + 1)
-            scan(r("SAf", 8 * a, 8 * b), r("VF", 16 * a, 16 * b, 2), r("VF", 16 * a + 1, 16 * b, 2), A.max, A.max)
-            if c == av:
-                ts(r("Qm"), r("pb", 0, K), 0.0, A.is_lt)
-                mm(r("pa", 0, K), r("N64"), r("Qm"), True, False)
-                if av:
-                    mm(r("pa", 0, CS), r("N1"), r("SBa", 15, 16 * CS, 16), False, False)
-                    mm(r("pa", 0, CS), r("Id"), r("SAa", 15, 16 * CS, 16), False, False)
-                mm(r("pa", av * CS, K), r("N1"), r("SBf", 8 * av * CS, 8 * K, 8), False, False)
-        mm(r("pa", av * CS, K), r("Id"), r("SAf", 8 * av * CS + 7, 8 * K, 8), False, True)
-        mm(r("pd", 0, NG), r(YW), r("Y", NV, WD), True, False)
-        if t == 0:
-            iota(r("MCA"), [[0, 12], [128, NBT]], 0)
-            iota(r("BIG", K, RO * K), [[ZMARK[2] - ZMARK[1], 2], [0, K]], ZMARK[1])
-            const(r("RWT", NBT, 112), 1 << 16)
-            wanted(None, 0, 2)
-            copy(r("PT2"), ind("PR", NX, "RLu", 0, 12))
-            tt(r("Y", *top), r("Y", *top), r("pa", 0, K), A.max)
-            absent(2, 3)
-            wanted(False, 2, 3)
+            act(r("Y", NV, WD), r("pa", 0, NG), F.Copy)
+            places()
         else:
+            copy(r("Y", NV, WD), r("pa", 0, NG))
+        n0 = av * CS
+        piece = lambda n, c, w=16: r(n, w * CS * c, w * CS * (c + 1))
+
+        def values(a, b):
+            act(r("VA", 16 * a, 16 * b), ind("Y", WY, "PTu", a, b), F.Copy)
+
+        def gathered(c):
+            tt(piece("VF", c), ind("Y", WY, "PTu", CS * c, CS * (c + 1)), r("OFF"), A.add)
+
+        def least(c):
+            a, b = CS * c, CS * (c + 1)
+            if c < av:
+                scan(piece("SBa", c), r("M1"), piece("VA", c), A.max, A.min)
+                mm(r("pb", a, b), r("Id"), r("SBa", 16 * a + 15, 16 * b, 16), True, True)
+            else:
+                scan(back("SBf", 8 * a, 8 * b, 1), back("VF", 16 * a, 16 * b, 2), back("VF", 16 * a, 16 * b - 1, 2), A.min, A.min, 4096.0)
+                mm(r("pb", a, b), r("Id"), r("SBf", 8 * a, 8 * b, 8), True, False)
+                mm(r("pb", a, b), r("N1"), r("OFF", 0, 16 * CS, 16), False, True)
+
+        def greatest(c):
+            a, b = CS * c, CS * (c + 1)
+            if c < av:
+                scan(piece("SAa", c), r("M0"), piece("VA", c), A.min, A.max)
+            else:
+                scan(piece("SAf", c, 8), r("VF", 16 * a, 16 * b, 2), r("VF", 16 * a + 1, 16 * b, 2), A.max, A.max)
+        lead = min(av, CFG["LEAD"]) if t else 1
+        for c in range(lead):
+            values(CS * c, CS * (c + 1))
+        if t and CFG["TUF"] == 1:
+            lists()
+            wait("first")
+        gathered(av)
+        if t and CFG["TUF"] == 0:
+            lists()
+        between = [lambda a=a: values(a, a + CS // 2) for a in range(CS * lead, n0, CS // 2)]
+        if t:
+            between += [lambda: act(r("OLD"), ind("Y", WY, "TLu", 0, 12), F.Copy),
+                        lambda: act(col("CB", 13 + 4 * t), col("CB", 12 + 4 * t), F.Identity, bias=col("CB", 4 * t - 4)),
+                        lambda: act(col("CB", 4 * t), col("Q", K), F.Identity, bias=col("CB", 13 + 4 * t), scale=-1.0)]
+        for f in between:
+            name_a()
+            f()
+        jp = CFG["JP"][t]
+        tail = ((1 if CFG["SGE"] else 0) + (2 if jp == 0 else 0)) if t else 0
+        name_a(max(0, na - at["A"] // 12 - tail))
+        for c in range(av + 1, K // CS):
+            gathered(c)
+            if t == 0 and c == K // CS - 1:
+                mm(r("pd", 0, NG), r(YW), r("Y", NV, WD), True, False)
+                absent(0, 2)
+                wanted(2)
+                mm(r("m2"), r("PW"), r(W, 1024, NV), True, False)
+            least(c - 1)
+        if t == 0:
+            greatest(av)
+        least(K // CS - 1)
+        wait("early")
+        mm(r("pa", 0, K), r("N1"), r("ZB", 0, K), True, False)
+        mm(r("pa", n0, K), r("N1"), r("SBf", 8 * n0, 8 * K, 8), False, False)
+        for c in range(av + (t == 0), K // CS):
+            greatest(c)
+        wait("early2")
+        mm(r("pa", n0, K), r("Id"), r("SAf", 8 * n0 + 7, 8 * K, 8), False, False)
+        for c in range(av):
+            least(c)
+            if c == av - 1:
+                mm(r("pa", 0, n0), r("N1"), r("SBa", 15, 16 * n0, 16), False, False)
+            greatest(c)
+        if av:
+            mm(r("pa", 0, n0), r("Id"), r("SAa", 15, 16 * n0, 16), False, False)
+        ts(r("Qm"), r("pb", 0, K), 0.0, A.is_lt)
+        mm(r("pa", 0, K), r("N64"), r("Qm"), False, True)
+
+        def computed(t=t):
+            act(r("JK"), r("Qm"), F.Identity, bias=1.0, scale=-1.0, acc=col("CB", 16 + 4 * t))
+
+        def surplus(t=t):
+            act(r("EB"), r("ONE"), F.Relu, bias=col("CB", 4 * t), scale=col("CB", 16 + 4 * t))
+        if jp == 0:
+            computed()
+            name_a()
+            surplus()
+            name_a()
+        if t == 0:
+            copy(r("PT2"), table(PR0, "RLu"))
+            copy(r("CTu"), table(CO0, "RLu"))
+            tt(r("Y", *top), r("Y", *top), r("pa", 0, K), A.max)
+            mm(r("m2"), r(YW), r("Y", 1024, NV), False, True)
+        else:
+            mm(r("pd", 0, NG), r(YW), r("Y", NV, WD), True, False)
+            wait("new")
             tt(r("NEW"), r("OLD"), r("pa", 0, K), A.max)
+            wait("put")
             copy(ind("Y", WY, "TLu", 0, 12), r("NEW"))
-            candidates(t, lambda: name("V", 1), lambda: absent(0, 2))
+            if CFG["SGE"]:
+                act(r("SG"), ind("Y", NV, "BDu", 0, 14), F.Sign, bias=0.5)
+                name_a()
+            if last:
+                for (a, b), s in (((0, S0), "s0"), (top, "s1")):
+                    dma("S", hbm(T.yy[:, a:b]), r("Y", a, b), s)
+            st = (ST * t) % RING
+            nb, first = NBR, S0 + st
+            wait("ring")
+            ts(r("HR", 0, RING - st), r("Y", S0 + st, S0 + RING), 0.0, A.is_ge)
+            ts(r("HR", RING - st, RING), r("Y", S0, S0 + st), 0.0, A.is_ge)
+            wait("count")
+            counted("HR", "RR", nb, 16 * nb)
+            for c in range(12):
+                a, b = c * nb, (c + 1) * nb
+                for u, w in ((a, min(b, 512)), (max(a, 512), b)):
+                    if u < w:
+                        mm(r("px", u, w), r("N4K"), r("RR", 8 * (u - a) + 7, 8 * (w - a), 8), False, w in (512, 12 * nb), inc=c == 11)
+            spread("RR", nb)
+            absent(0, 2)
+            wait("block")
+            scan(back("FS", 0, 12 * nb, 1), back("px", 0, 12 * nb, 1), back(("B1", "MCB")[t - 1], 0, 12 * nb, 1), A.min, A.max, float(first + 16 * nb))
+            copy(r("RWR", 0, nb), r("pb", 0, nb))
+            wait("place")
+            bl = r("FS", 0, 12 * nb, nb)
+            ts(r("Bu", 0, 12), bl, -float(first), A.add, 1.0 / 16, A.mult)
+            ts(r("BB", 0, 12), bl, S0 + RING - 0.5, A.is_ge, -float(RING), A.mult)
+            ts(r("BC", 0, 12), bl, first + RING - 0.5, A.is_ge, float(RING + TOP - st), A.mult)
+            tt(r("F2"), ind("RWR", 80, "Bu", 0, 12), r("I16"), A.is_le)
+            inside([bl, r("BB", 0, 12)], [r("BC", 0, 12)])
+            wait("list")
+            copy(r("RLu", 0, 12), r("pc", 0, 12))
             absent(2, 3)
-            copy(r("PT2"), ind("PR", NX, "RLu", 0, 12))
-            name("V", 16)
-            wanted(None, 0, 3)
-        dg, hg = CFG["DG"][t], CFG["HG"][t]
+            name_v(K)
+            wanted(3)
+            copy(r("PT2"), table(PR0, "RLu"))
+            copy(r("CTu"), table(CO0, "RLu"))
+        dg, hg = CFG["DG"], CFG["HG"][t]
         act(r("OL2"), ind("Y", WY, "RLu", 0, 12), F.Copy)
         for i in range(3):
             act(r("DG", 16 * dg[i], 16 * dg[i + 1]), ind("Y", WY, "PT2", dg[i], dg[i + 1]), F.Relu, scale=-1.0)
-            if i == 0:
+            if i == 0 and not (t and CFG["SGE"]):
                 act(r("SG"), ind("Y", NV, "BDu", 0, 14), F.Sign, bias=0.5)
-        copy(r("CTu"), ind("CO", NX, "RLu", 0, 12))
-        if dg[3] < K:
-            ts(r("DG", 16 * dg[3], 16 * K), ind("Y", WY, "PT2", dg[3], K), 0.0, A.is_lt)
         tt(r("NS%d" % t), r("pd", 0, NG), r("Z", NV, WD), A.is_ge)
         send("NS%d" % t, "LN%d" % t, "an%d" % t, "on%d" % t)
         if t == 0:
-            for u in (2, 3):
-                const(r("W%d" % u, NV, WD), 0)
-                const(r("W%d" % u, WD, WY), 1)
-            const(r("OW", NV, NX), 0)
-        for j in range(3):
-            tt(r(Wn, 512 * j, 512 * (j + 1)), r("m%d" % j), r("Z", 512 * j, 512 * (j + 1)), A.is_ge)
+            const(r("TAB", MO0 + NV - TOP, MO0 + NX), 0)
+            const(r("Q", 0, 16), 0)
+            for n in ("NH", "NE", "N8"):
+                diag(n)
+            select(r("BO"), r("ONE", 0, 128), [[-16, 8], [0, 16]], A.is_ge, 0.0, 0)
+            select(r("BO"), r("BO"), [[16, 8], [0, 16]], A.is_ge, 0.0, 15, -1)
+            iota(r("MCA", 0, (12 - CFG["CA"]) * NBT), [[0, 12 - CFG["CA"]], [128, NBT]], 0)
+            const(r("RWT", NBT, 112), 1 << 16)
+            const(r("ON5"), 1)
+        tt(r(Wn, 0, NV), r("pm"), r("Z", 0, NV), A.is_ge)
         hw = WD + 16
+
+        def consumers(i):
+            copy(r("HG", 16 * hg[i], 16 * hg[i + 1]), ind(Wn, hw, "CTu", hg[i], hg[i + 1]))
+        act(r("WB"), ind(Wn, NV, "BDu", 0, 14), F.Copy)
+        act(r("HG", 16 * hg[4], 16 * K), ind(Wn, hw, "CTu", hg[4], K), F.Copy)
         ksum("pd", "DG", 0, dg[1])
         mm(r("pa", 0, NG), r("NH"), r("SG"), True, False)
         mm(r("pa", 0, NG), r("NE"), r("SG"), False, False)
-        tt(r("OI"), ind("MO", NX, "RLu", 0, 12), r("OL2"), A.mult)
-        copy(r("HG", 0, 16 * hg[1]), ind(Wn, hw, "CTu", 0, hg[1]))
+        mm(r("m0", 0, K), r("N1"), r("ONE"), True, False)
+        mm(r("m0", 0, K), r("N1"), r("OL2"), False, False)
+        tt(r("OI"), table(MO0, "RLu"), r("OL2"), A.mult)
+        consumers(0)
         ksum("pd", "DG", dg[1], dg[2])
         ksum("ph", "HG", 0, hg[1])
         ts(r("OM"), r("OI"), 1, A.bitwise_and)
-        copy(r("HG", 16 * hg[1], 16 * hg[2]), ind(Wn, hw, "CTu", hg[1], hg[2]))
+        consumers(1)
         ksum("pd", "DG", dg[2], K)
-        ksum("ph", "HG", hg[1], hg[2])
-        act(r("JK"), r("Qm"), F.Identity, bias=1.0, scale=-1.0, acc=col("CB", 16 + 4 * t))
-        if hg[3] < K:
-            act(r("HG", 16 * hg[3], 16 * K), ind(Wn, hw, "CTu", hg[3], K), F.Copy)
-        act(r("EB"), r("ONE"), F.Relu, bias=col("CB", 4 * t), scale=col("CB", 16 + 4 * t))
+        mm(r("pa", 0, NG), r("N1"), r("WB"), False, False)
         facing("LN%d" % t, False)
-        act(r("NF"), r("pa", 0, NG), F.Identity, bias=EPS / 2 - 0.5)
-        if CFG["FF"][t]:
-            tt(r("Ff"), r("OM"), r("pd", 0, K), A.min)
-        copy(r("HG", 16 * hg[2], 16 * hg[3]), ind(Wn, hw, "CTu", hg[2], hg[3]))
-        if not CFG["FF"][t]:
-            ksum("ph", "HG", hg[2], K)
-            tt(r("Ff"), r("OM"), r("pd", 0, K), A.min)
+        ksum("ph", "HG", hg[1], hg[2])
+        if jp == 2:
+            computed()
+        act(r("NF"), r("pa", 0, NG), F.Relu, bias=EPS / 2 - 0.5)
+        if jp == 1:
+            computed()
+        if jp == 2:
+            surplus()
+        consumers(2)
+        tt(r("Ff"), r("OM"), r("pd", 0, K), A.min)
         mm(r("pb", 0, K), r("BO"), r("Ff"), True, True)
-        if CFG["FF"][t]:
-            ksum("ph", "HG", hg[2], K)
-        mm(r("pd", 0, K), r("N1"), r("ONE"), True, False)
-        mm(r("pd", 0, K), r("N8"), r("Ff"), False, False)
-        mm(r("pd", 0, K), r("N1"), r("OL2"), False, True)
-        if CFG["FF"][t]:
-            act(r("AB"), r("pb", 0, K), F.Abs, bias=-8.0)
+        mm(r("m0", 0, K), r("N8"), r("Ff"), False, True)
+        if hg[4] > hg[3]:
+            consumers(3)
+        ksum("ph", "HG", hg[2], K)
+        act(r("AB"), r("pb", 0, K), F.Abs, bias=-8.0)
+        if jp == 1:
+            surplus()
+        if CFG["RWV"]:
             act(r("TH"), r("AB"), F.Identity, bias=EPS / 2 - 8.0)
+        else:
+            mm(r("m1", 0, K), r("N1"), r("AB"), True, False)
         act(r("FR"), r("ph", 0, K), F.Relu, bias=1.0, scale=-1.0)
-        if not CFG["FF"][t]:
-            act(r("AB"), r("pb", 0, K), F.Abs, bias=-8.0)
-            act(r("TH"), r("AB"), F.Identity, bias=EPS / 2 - 8.0)
-        if not last:
-            act(col("CB", 17 + 4 * t), col("CB", 16 + 4 * t), F.Identity, bias=col("CB", 4 * t))
-        if last:
-            for (a, b), s1, s2 in (((0, S0), "s0", "s1"), (top, "s2", "s3")):
-                ts(r("OY", a, b), r("Y", a, b), -1.0, A.max)
-                dma("S", hbm(T.yy[:, a:b]), r("OY", a, b), s1)
-                ts(r("OF", a, b), r("Y", a, b), -1.0625, A.is_lt)
-                dma("S", hbm(T.yf[:, a:b]), r("OF", a, b), s2)
-        tt(r("NT"), ind(Wn, NV, "BDu", 0, 14), r("NF"), A.max)
-        copy(ind(Wn, NV, "BDu", 0, 14), r("NT"))
-        scan(r("Q", 1, K + 1), r("FR"), r("EB"), A.add, A.min)
+        tt(ind(Wn, NV, "BDu", 0, 14), r("NF"), r("WB"), A.add)
+        if not CFG["RWV"]:
+            act(r("TH"), ind(Wn, WY, "RLu", 0, 12), F.Copy, scale=1.0 / EPS)
+            mm(r("m1", 0, K), r("Id"), r("TH"), False, True)
         if last:
             act(r("OW", 0, NV), r(Wn, 0, NV), F.Relu, bias=-0.003, scale=1.003)
+        if not CFG["RWV"]:
+            act(r("RW2"), r("m1", 0, K), F.Sign, bias=8.0)
+        scan(r("Q", 1, K + 1), r("FR"), r("EB"), A.add, A.min)
+        if CFG["RWV"]:
+            tt(r("RW2"), ind(Wn, WY, "RLu", 0, 12), r("TH"), A.is_gt)
         scan(r("GO"), r("Q", 1, K + 1), r("Q", 0, K), A.max, A.subtract)
-        tt(r("RW2"), ind(Wn, WY, "RLu", 0, 12), r("TH"), A.is_gt)
-        scan(r("TA"), r("GO"), r("pd", 0, K), A.max, A.mult)
+
+        def rewant():
+            tt(ind(Wn, WY, "RLu", 0, 12), r("GO"), r("RW2"), A.mult)
+        if CFG["TO"] == 1 and not last:
+            rewant()
+        scan(r("TA"), r("GO"), r("m0", 0, K), A.max, A.mult)
+        if CFG["TO"] == 2 and not last:
+            rewant()
+        if CFG["TO"] == 1 and not last:
+            counted(Wn, "R", NBT, NV)
         tt(ind("Y", WY, "RLu", 0, 12), r("TA"), r("OL2"), A.add)
         if not last:
             act(r("G%d" % (t + 1)), ind("Y", NV, "BDu", 0, 14), F.Copy)
             send("G%d" % (t + 1), "LG%d" % (t + 1), "ag%d" % (t + 1), "og%d" % (t + 1))
-            tt(ind(Wn, WY, "RLu", 0, 12), r("GO"), r("RW2"), A.mult)
-            act(col("CB", 4 * t + 4), col("Q", K), F.Identity, bias=col("CB", 17 + 4 * t), scale=-1.0)
+            if t == 0:
+                iota(r("BIG", K, RO * K), [[ZMARK[2] - ZMARK[1], 2], [0, K]], ZMARK[1])
+                iota(r("T1"), [[16, 12], [0, NBR]], 0)
+                for n in ("P4K", "N4K", "Y1"):
+                    diag(n)
+                iota(r("B1"), [[0, 12], [16, NBR]], S0 + ST % RING)
+            else:
+                diag("Y2")
+                iota(r("MCB"), [[0, 12], [16, NBR]], S0 + 2 * ST % RING)
+                const(r("OW", NV, NX), 0)
+            const(r("W%d" % (t + 2), NV, WD), 0)
+            const(r("W%d" % (t + 2), WD, WY), 1)
+            if CFG["TO"] == 0:
+                rewant()
+            if CFG["TO"] != 1:
+                counted(Wn, "R", NBT, NV)
         else:
             ts(r("OY", *ring), r("Y", *ring), -1.0, A.max)
             dma("S", hbm(T.yy[:, ring[0]:ring[1]]), r("OY", *ring), "s4")
             ts(r("OF", *ring), r("Y", *ring), -1.0625, A.is_lt)
-            dma("A", hbm(T.yf[:, ring[0]:ring[1]]), r("OF", *ring), "s5")
+            dma("S", hbm(T.yf[:, ring[0]:ring[1]]), r("OF", *ring), "s5")
             tt(ind("OW", NX, "RLu", 0, 12), r("GO"), r("RW2"), A.mult)
             dma("S", hbm(T.yw[:, :]), (T.OW[0:128:16, 0:NV], [("OW", 0, NV)], []), "s6")
     return ops, Q

from concourse.bass import DstId, RemoteDMATransfer
from concourse.mybir import AluOpType as A, ActivationFunctionType as F

NV, S0, TOP, GH, K, LIM, ST, RO = 1536, 384, 192, 32, 192, 704, 432, 3
RING = NV - S0 - TOP
NG = 7 * GH
WD = NV + NG
WY = WD + K
NX = NV + K
PR0, CO0, MO0 = 0, NX - S0, 2 * (NX - S0)
CS = 48
NBT, NBR = NV // 16, (RING + K) // 16
B16, F16, F32, I32, U16 = "bfloat16", "float16", "float32", "int32", "uint16"
EPS = 2.0 ** -9
ZMARK, ZNONE, WW, WYS = (30, 24, 18), 35.0, 15.5, (30.25, 25.0, 20.0)


def sb(n, d):
    return ("sbuf", [128, n], d)


SCRATCH = {
    "Y": sb(WY, B16), "TAB": sb(MO0 + NX, I32), "BD": sb(16, I32), "BDu": sb(16, U16),
    "Z": sb(WY, F32), "ZC": sb(WY // 4, F32), "RR": sb(NX // 2, F16), "ZB": sb(S0, B16), "H0": sb(K, B16),
    "VA": sb(48 * CS, B16), "SAa": sb(48 * CS, B16), "SBa": sb(48 * CS, B16), "M0": sb(16 * CS, B16), "M1": sb(16 * CS, B16),
    "VF": sb(16 * K, F16), "SAf": sb(8 * K, F16), "SBf": sb(8 * K, F16), "OFF": sb(16 * CS, B16),
    "DG": sb(16 * K, B16), "HG": sb(16 * K, B16), "ON5": sb(512, B16), "T1": sb(12 * NBR, B16), "B1": sb(12 * NBR, B16),
    "MCA": sb(12 * NBT, B16), "MCB": sb(12 * NBR, B16), "FC": sb(12 * NBT, B16), "FS": sb(12 * NBT, B16),
    "R": sb(NV // 2, B16), "HR": sb(NX, B16), "RWT": sb(112, F32), "RWR": sb(80, F32),
    "F2": sb(K, B16), "Bu": sb(16, U16), "BA": sb(16, B16), "BB": sb(16, B16), "BC": sb(16, B16), "BF": sb(16, B16),
    "TLu": sb(16, U16), "RLu": sb(16, U16), "SEL": sb(16, U16),
    "PTu": sb(K, U16), "PT2": sb(K, U16), "CTu": sb(K, U16), "TU": sb(K, U16), "P": sb(K + 32, F32), "TT": sb(2 * K + 32, F32),
    "OLD": sb(K, B16), "OL2": sb(K, B16), "Qm": sb(K, B16), "NEW": sb(K, B16), "OI": sb(K, I32), "OM": sb(K, I32),
    "Ff": sb(K, B16), "AB": sb(K, B16), "TH": sb(K, B16), "RW2": sb(K, B16), "FR": sb(K, B16),
    "Q": sb(208, B16), "GO": sb(K, B16), "TA": sb(K, B16), "EB": sb(K, B16), "JK": sb(K, B16), "JL": sb(K, B16),
    "SG": sb(NG, B16), "NF": sb(NG, B16), "WB": sb(NG, B16),
    "ONE": sb(K, B16), "BIG": sb(RO * K, F32), "I16": sb(K, F32), "X0": sb(K, F32),
    "IP": sb(4, I32), "IM": sb(144, F32), "J": sb(12, F32), "SL": sb(12, F32), "CI": sb(64, I32), "CF": sb(128, F32),
    "SH": sb(12, F32), "BS": sb(12, F32), "CB": sb(32, F32),
    "XB": sb(144, B16), "XN": sb(144, B16), "X2": sb(144, B16), "OY": sb(NV, B16), "OF": sb(NV, B16), "OW": sb(NX, B16),
}
DIAG = {"Id": 1.0, "N1": -1.0, "N8": -0.125, "N64": -64.0, "NH": -0.5, "NE": EPS / 2, "PW": WW, "Y0": -WYS[0], "Y1": -WYS[1], "Y2": -WYS[2],
        "P4K": 4096.0, "N4K": -4096.0}
for _n in list(DIAG) + ["P1", "P2", "BO", "DSH"]:
    SCRATCH[_n] = sb(128, B16)
for _t in range(RO + 1):
    SCRATCH["W%d" % _t] = sb(WY, B16)
for _t in range(RO):
    for _n in ("G", "NS", "LG", "LN"):
        SCRATCH["%s%d" % (_n, _t)] = sb(NG, B16)
BANKS = {"m0": ("pm", 0), "m1": ("pm", 512), "m2": ("pm", 1024), "pc": ("px", 0), "ph": ("px", 512), "pa": ("pa", 0), "pb": ("pb", 0), "pd": ("pd", 0)}
for _n, _w in (("pm", 1536), ("px", 1024), ("pa", 512), ("pb", 512), ("pd", 512)):
    SCRATCH[_n] = ("psum", [128, _w], F32)

SEMAPHORES = (["qV", "qA", "qP", "qG", "ly", "lb", "lt", "lp", "lq", "lc", "lm", "s0", "s1", "s2", "s3", "s4", "s5", "s6"]
              + ["%s%d" % (n, t) for n in ("ag", "an", "og", "on") for t in range(RO)])

CFG = {
    "NA": (13, 10, 10),
    "AV": (1, 3, 3),
    "PRE": 7,
    "TUF": 0, "AQ": 1, "JP": (1, 1, 1),
    "VW": {"first": 0, "early": 0, "early2": 0, "new": 12, "put": 4, "ring": 8, "count": 4, "block": 20, "place": 12, "list": 12, "cand": 0},
    "CA": 5,
    "DG": (0, 64, 128, 192),
    "HG": ((0, 64, 128, 152, 172), (0, 64, 128, 144, 156), (0, 64, 128, 144, 156)),
    "RWV": 0, "PG": 2, "TO": 0, "SGE": 1, "LEAD": 3,
}


def build(g, core, T, topo):
    rank = T.rank_of(core)
    ops = []
    Q = {"V": g.vector, "A": g.scalar, "P": g.tensor, "G": g, "S": g.sync}

    def touched(name, a, b):
        if name in ("pm", "px"):
            return [(n, 0, 512) for n in BANKS if BANKS[n][0] == name and BANKS[n][1] < b and a < BANKS[n][1] + 512]
        return [(name, a, b)]

    def r(name, a=None, b=None, s=None):
        a = 0 if a is None else a
        if name in BANKS:
            t, o = T[BANKS[name][0]], BANKS[name][1]
            b = 512 if b is None else b
            return (t[:, o + a:o + b:s or 1], [(name, a, b)], [])
        t = T[name]
        b = t.shape[1] if b is None else b
        return (t[:, a:b] if s is None else t[:, a:b:s], touched(name, a, b), [])

    def back(name, a, b, s):
        t = T[name]
        return (t[:, b - 1::-s] if a == 0 else t[:, b - 1:a - 1:-s], touched(name, a, b), [])

    def ind(name, b, off, c, d):
        return (T[name][:, 0:b].indirect(T[off][:, c:d]), [(name, 0, b)], [(off, c, d)])

    def table(a, off):
        return (T.TAB[:, a:a + NX].indirect(T[off][:, 0:12]), [("TAB", a, a + NX)], [(off, 0, 12)])

    def op(q, fn, out, ins, sem=None, inc=True, cnt=16):
        rd = []
        for x in ins:
            if isinstance(x, tuple):
                rd += x[1] + x[2]
        wr = []
        if out is not None:
            wr = out[1]
            rd += out[2]
        ops.append({"q": q, "fn": fn, "rd": rd, "wr": wr, "sem": sem, "inc": inc, "cnt": cnt})

    def v(x):
        return x[0] if isinstance(x, tuple) else x

    def copy(o, i):
        op("V", lambda: g.vector.tensor_copy(o[0], i[0]), o, [i])

    def tt(o, a, b, f):
        op("V", lambda: g.vector.tensor_tensor(o[0], a[0], b[0], f), o, [a, b])

    def ts(o, a, s1, f1, s2=None, f2=None):
        if f2 is None:
            op("V", lambda: g.vector.tensor_scalar(o[0], a[0], v(s1), None, f1), o, [a, s1])
        else:
            op("V", lambda: g.vector.tensor_scalar(o[0], a[0], v(s1), v(s2), f1, f2), o, [a, s1, s2])

    def scan(o, a, b, f1, f2, init=0.0):
        op("V", lambda: g.vector.tensor_tensor_scan(o[0], a[0], b[0], init, f1, f2), o, [a, b])

    def fill(o, c):
        op("V", lambda: g.vector.memset(o[0], c), o, [])

    def tr(o, i):
        op("V", lambda: g.vector.transpose(o[0], i[0]), o, [i])

    def act(o, i, f, bias=0.0, scale=1.0, acc=None):
        oo = o if acc is None else (o[0], o[1] + acc[1], o[2])
        if acc is None:
            op("A", lambda: g.scalar.activation(o[0], i[0], f, bias=v(bias), scale=v(scale)), oo, [i, bias, scale])
        else:
            op("A", lambda: g.scalar.activation(o[0], i[0], f, bias=v(bias), scale=v(scale), accum_out=acc[0]), oo, [i, bias, scale])

    def silu(o, i):
        op("A", lambda: g.scalar.activation(o[0], i[0], F.Silu), o, [i])

    def mm(o, l, x, start, stop, inc=None):
        op("P", lambda: g.tensor.matmul(o[0], l[0], x[0], start, stop), o, [l, x], inc=stop if inc is None else inc)

    def iota(o, pat, base, cm=0):
        if SCRATCH[o[1][0][0]][2] == I32:
            op("G", lambda: g.iota(o[0], pat, base, cm), o, [])
        else:
            op("G", lambda: g.iota(o[0], pat, base, cm, allow_small_or_imprecise_dtypes=True), o, [])

    def const(o, c):
        iota(o, [[0, o[1][0][2] - o[1][0][1]]], c)

    def select(o, i, pat, f, c, base, cm=1):
        op("G", lambda: g.affine_select(o[0], i[0], pat, f, c, base, cm), o, [i])

    def diag(n):
        select(r(n), r("ZB", 0, 128), [[-1, 128]], A.not_equal, DIAG[n], 0)

    def dma(q, o, i, sem, extra=()):
        op(q, lambda: Q[q].dma_start(o[0], i[0]), o, [i] + list(extra), sem=sem)

    def hbm(ap):
        return (ap, [], [])

    def send(src, dst, arr, out):
        def fn():
            trs = []
            for d in range(1, len(T.cores)):
                to = T.cores[rank ^ d]
                rid, pid = topo.addr(to)[:2]
                eng = topo.engines(core, to)
                trs.append(RemoteDMATransfer(dst_ids=[DstId(rid=rid, pnc=pid)], dma_engine_mask=1 << eng[(d - 1) % len(eng)],
                                             remote_sem=T.sem[arr], src=T[src][:, (d - 1) * GH:d * GH], dst=T[dst][:, (d - 1) * GH:d * GH]))
            g.remote_dma_fused(trs, local_sem=T.sem[out])
            return None
        op("G", fn, (None, [("sent" + out, 0, 1)], []), [r(src)], sem=out, cnt=7)
        op("X", None, r(dst), [], sem=arr, cnt=7)

    def col(name, j):
        return r(name, j, j + 1)

    perm = ("P1", "P2", "Id")
    top, ring = (NV - TOP, NV), (S0, NV - TOP)

    dma("S", r("Y", 0, NV), hbm(T.y0[:, :]), "ly")
    dma("A", r("BD", 0, 14), hbm(T.bd[:, :]), "lb")
    dma("A", r("TAB", *top), hbm(T.pr[:, top[0]:top[1]]), "lt")
    iota(col("IP", 0), [[0, 1]], 0, 1)
    iota(r("J"), [[16, 12]], 0)
    iota(r("IM"), [[1, 144]], 0)
    iota(r("TAB", NV, NX), [[1, K]], WD)
    const(r("P", 0, 16), 0)
    const(r("P", K + 16, K + 32), 0)
    const(r("Z", WY // 4 * 3, WY), int(ZNONE))
    fill(r("ZC"), ZNONE)
    for i in range(3):
        silu(r("Z", WY // 4 * i, WY // 4 * (i + 1)), r("ZC"))
    fill(r("ZB"), 0.0)
    for a, b in ((0, 336), (336, 672), (672, 1008), (1008, NV - TOP), (NV, NV + 208), (NV + 208, WY)):
        dma("S", r("W0", a, b), r("ZB", 0, b - a), "lp", [r("Y", 0, NV)])
    ci = lambda j, n=1: r("CI", 4 * j, 4 * j + n)
    cf = lambda j, n=1: r("CF", 4 * j, 4 * j + n)
    ts(ci(0), col("IP", 0), 15, A.bitwise_and)
    ts(ci(1), col("IP", 0), 16, A.bitwise_and)
    copy(cf(0), col("IP", 0))
    copy(cf(1), ci(0))
    copy(cf(2), ci(1))
    ts(r("SL"), r("J"), cf(1), A.add)
    ts(cf(3), cf(0), cf(1), A.subtract)
    ts(cf(7), cf(2), -2.0, A.mult, 32.0, A.add)
    ts(cf(8, 12), r("SL"), 1.0 / 12, A.mult, 0.5 / 12 - 0.5, A.add)
    ts(r("XB"), r("IM"), cf(3), A.subtract, 15.0, A.is_equal)
    ts(cf(16, 12), r("SL"), 32.0, A.mult, cf(2), A.add)
    copy(ci(8, 12), cf(8, 12))
    ts(r("XN"), r("XB"), -1.0, A.mult)
    ts(r("SH"), r("SL"), 0.75, A.add)
    ts(cf(24, 12), ci(8, 12), 12.0, A.mult, 5.5, A.add)
    ts(cf(12, 12), ci(8, 12), -383.0, A.mult)
    scan(r("X2", 0, 143), r("XB", 0, 143), r("XB", 1, 144), A.min, A.add, 1.0)
    tt(cf(28, 12), r("SL"), cf(24, 12), A.is_ge)
    tt(cf(20, 12), cf(12, 12), cf(16, 12), A.add)
    copy(r("BDu", 0, 14), r("BD", 0, 14))
    ts(cf(24, 12), cf(28, 12), cf(7), A.mult)

    def counted(row, run, nb, n):
        for j in range(8):
            mm(r("pb", 0, nb), r("XN", 15 - 2 * j, 143 - 2 * j), r(row, 2 * j + 1, 16 * nb, 16), j == 0, False)
        scan(r(run, 0, n // 2), r(row, 0, n, 2), r(row, 1, n, 2), A.add, A.add)

    def spread(run, nb):
        for j in range(8):
            mm(r("pb", 0, nb), r("X2", 14 - 2 * j, 142 - 2 * j), r(run, j, 8 * nb, 8), False, j == 7)

    def blocks(run, nb, mask, rw, na):
        nv = 12 - na
        ends = r(run, 7, 8 * nb, 8)
        spread(run, nb)
        for b in range(nv, 12):
            act(r("JK" if b % 2 else "JL", 0, nb), ends, F.Sign, bias=col("SH", b), scale=-1.0, acc=col("BS", b))
        for b in range(nv):
            ts(r("FC", b * nb, (b + 1) * nb), ends, col("SH", b), A.is_le)
        if na:
            act(r(rw, 0, nb), r("pb", 0, nb), F.Copy)
        else:
            copy(r(rw, 0, nb), r("pb", 0, nb))
        if mask:
            scan(r("FS", 0, nv * nb), r(mask, 0, nv * nb), r("FC", 0, nv * nb), A.min, A.add)
            ts(r("Bu", nv, 12), r("BS", nv, 12), 0.5, A.mult, nb / 2, A.add)
            bl = r("FS", nb - 1, nv * nb, nb)
        else:
            h = nb // 2
            scan(r("SAf", 16, 16 + 12 * h), r("FC", 0, 12 * nb, 2), r("FC", 1, 12 * nb, 2), A.add, A.add)
            ts(r("W0", *top), r("Y", *top), 0.0, A.is_lt)
            ts(col("CB", 0), col("RR", NX // 2 - 1), -float(K + LIM), A.add)
            bl = r("BF", 0, 12)
            tt(bl, r("SAf", 15 + h, 16 + 12 * h, h), r("SAf", 15, 16 + 11 * h, h), A.subtract)
            copy(r("PTu"), r("P", 16, K + 16))
        copy(r("Bu", 0, nv), bl)
        return bl

    def inside(first, rest):
        for i, x in enumerate(first):
            mm(r("pc", 0, 12), r("Id"), x, i == 0, False)
        for a in range(16):
            mm(r("pc", 0, 12), r("XB", 15 - a, 143 - a), r("F2", a, K, 16), a == 0 and not first, False)
        for i, x in enumerate(rest):
            mm(r("pc", 0, 12), r("Id"), x, False, i == len(rest) - 1)

    def places():
        for a, b in ((0, 512), (512, 12 * NBR)):
            mm(r("px", a, b), r("P4K"), r("T1", a, b), True, False)
            mm(r("px", a, b), r("DSH"), r("ON5", 0, b - a), False, False)

    def ksum(bank, src, a, b):
        for k in range(16):
            mm(r(bank, a, b), r("Id"), r(src, 16 * a + k, 16 * b, 16), k == 0, k == 15)

    def facing(src, first):
        for d in range(1, 8):
            mm(r("pa", (d - 1) * GH, d * GH), r(perm[(d - 1) % 3]), r(src, (d - 1) * GH, d * GH), first, first or d == 7, inc=d == 7)

    for t in range(RO):
        W, Wn, YW = "W%d" % t, "W%d" % (t + 1), "Y%d" % t
        last = t == RO - 1
        na, av = CFG["NA"][t], CFG["AV"][t]
        at = {"A": 0, "V": 12 * na}

        def name_a(n=1, at=at, na=na, t=t):
            for _ in range(n):
                if at["A"] < 12 * na:
                    silu(ind("Z", WY, "TU", at["A"], at["A"] + 12), r("BIG", t * K, (t + 1) * K))
                    at["A"] += 12

        def name_v(n, at=at, W=W):
            while n > 0 and at["V"] < K:
                c = at["V"]
                d = min(c + n, c // 12 * 12 + 12)
                copy(ind(W, WY, "TU", c, d), r("ONE", 0, 16 * (d - c)))
                at["V"], n = d, n - (d - c)

        def wait(where, t=t):
            if t:
                name_v(CFG["VW"][where])

        def absent(a, b, YW=YW):
            for j in range(a, b):
                mm(r("m%d" % j), r(YW), r("Y", 512 * j, 512 * (j + 1)), True, False)

        def wanted(b, W=W):
            mm(r("pd", 0, NG), r("PW"), r(W, NV, WD), False, True)
            for j in range(b):
                mm(r("m%d" % j), r("PW"), r(W, 512 * j, 512 * (j + 1)), False, True)

        def turn():
            tr(r("TT", 0, K), r("P", 16, K + 16))
            tr(r("TT", K, 2 * K + 32), r("P"))

        def lists():
            copy(r("TU"), ind("TT", 2 * K + 32, "SEL", 0, 12))

        if t == 0:
            ts(r("H0"), r("Y", *top), 0.0, A.is_ge, 4096.0, A.mult)
            copy(r("G0"), ind("Y", NV, "BDu", 0, 14))
            send("G0", "LG0", "ag0", "og0")
            tt(r("X0"), r("TAB", *top), r("H0"), A.add)
            tt(cf(28, 12), cf(24, 12), cf(20, 12), A.add)
            ts(r("HR", RING + K, RING + K + S0), r("Y", 0, S0), 0.0, A.is_ge)
            const(r("BIG", 0, K), ZMARK[0])
            tt(r("P", 16, K + 16), r("X0"), r("TAB", NV, NX), A.min)
            copy(r("SEL", 0, 12), cf(28, 12))
            ts(r("HR", RING + K + S0, NX), r("Y", *top), 0.0, A.is_ge)
            turn()
            ts(r("HR", 0, RING), r("Y", *ring), 0.0, A.is_ge)
            lists()
            name_a(CFG["PRE"])
            const(r("HR", RING, RING + K), 1)
            iota(r("I16"), [[16, K]], 12)
            const(r("RWR", NBR, 80), 0)
            diag("Id")
            const(r("ONE"), 1)
            select(r("P1"), r("ZB", 0, 128), [[16, 8], [-1, 16]], A.not_equal, 1.0, -112)
            select(r("P2", 0, 16), r("ZB", 0, 16), [[-1, 16]], A.not_equal, 1.0, 0)
            select(r("P2", 16, 128), r("ZB", 0, 112), [[16, 7], [-1, 16]], A.not_equal, 1.0, -112)
            const(r("Y", WD, WY), -1)
            iota(r("OFF"), [[32, CS], [0, 16]], 32)
            diag("N1")
            diag("Y0")
            diag("PW")
            iota(r("M1"), [[0, CS], [-32, 16]], 20)
            iota(r("M0"), [[0, CS], [32, 16]], 0)
            diag("N64")
            counted("HR", "RR", NBR, NX)
            copy(r("SAf", 0, 16), r("ZB", 0, 16))
            bl = blocks("RR", NBR, None, "RWR", 0)
            ts(r("BA", 0, 12), bl, 16.0, A.mult, float(S0), A.add)
            ts(r("BB", 0, 12), bl, RING // 16 - 0.5, A.is_ge, float(TOP), A.mult)
            tt(r("F2"), ind("RWR", 80, "Bu", 0, 12), r("I16"), A.is_le)
            inside([], [r("BA", 0, 12), r("BB", 0, 12)])
            name_v(12)
            copy(r("RLu", 0, 12), r("pc", 0, 12))
            after = [(None, [("sentog0", 0, 1)], [])]
            dma("S", r("TAB", PR0, PR0 + NV - TOP), hbm(T.pr[:, 0:NV - TOP]), "lq", after)
            dma("S", r("TAB", CO0 + ring[0], CO0 + ring[1]), hbm(T.co[:, ring[0]:ring[1]]), "lc")
            for k in range(16):
                a, b = MO0 + ring[0], MO0 + ring[1]
                dma("S", (T.TAB[k:128:16, a:b], [("TAB", a, b)], []), hbm(T.mo[:, ring[0]:ring[1]]), "lm")
            for (a, b), s in (((0, S0), "s2"), (top, "s3")):
                dma("S", hbm(T.yf[:, a:b]), r("ZB", 0, b - a), s)
            const(r("TAB", CO0 + NV - TOP, CO0 + NX), WD)
            const(r("W1", NV, WD), 0)
            const(r("W1", WD, WY), 1)
            name_v(K)
        else:
            blocks("R", NBT, "MCA", "RWT", CFG["CA"])
            tt(r("F2"), ind("RWT", 112, "Bu", 0, 12), r("I16"), A.is_le)
            ts(r("BF", 0, 12), r("Bu", 0, 12), NBT - 0.5, A.is_ge)
            ts(r("BA", 0, 12), r("Bu", 0, 12), 16.0, A.mult)
            tt(r("BB", 0, 12), r("BF", 0, 12), r("SL"), A.mult)
            inside([], [r("BA", 0, 12), r("BB", 0, 12)])
            copy(r("TLu", 0, 12), r("pc", 0, 12))
            if t == 1:
                act(col("CB", 31), col("SH", 0), F.Copy, scale=4096.0)
                act(r("DSH"), r("Id"), F.Copy, scale=col("CB", 31))
            if CFG["PG"] == 2:
                copy(r("P", 16, K + 16), table(PR0, "TLu"))
            copy(r("PTu"), table(PR0, "TLu"))
            if CFG["PG"] == 1:
                copy(r("P", 16, K + 16), table(PR0, "TLu"))
            if CFG["PG"] == 0:
                copy(r("P", 16, K + 16), r("PTu"))
            turn()
            if CFG["TUF"] == 2:
                lists()
                name_a(CFG["AQ"])
                wait("first")
        facing("LG%d" % t, True)
        if t:
            act(r("Y", NV, WD), r("pa", 0, NG), F.Copy)
            places()
        else:
            copy(r("Y", NV, WD), r("pa", 0, NG))
        n0 = av * CS
        piece = lambda n, c, w=16: r(n, w * CS * c, w * CS * (c + 1))

        def values(a, b):
            act(r("VA", 16 * a, 16 * b), ind("Y", WY, "PTu", a, b), F.Copy)

        def gathered(c):
            tt(piece("VF", c), ind("Y", WY, "PTu", CS * c, CS * (c + 1)), r("OFF"), A.add)

        def least(c):
            a, b = CS * c, CS * (c + 1)
            if c < av:
                scan(piece("SBa", c), r("M1"), piece("VA", c), A.max, A.min)
                mm(r("pb", a, b), r("Id"), r("SBa", 16 * a + 15, 16 * b, 16), True, True)
            else:
                scan(back("SBf", 8 * a, 8 * b, 1), back("VF", 16 * a, 16 * b, 2), back("VF", 16 * a, 16 * b - 1, 2), A.min, A.min, 4096.0)
                mm(r("pb", a, b), r("Id"), r("SBf", 8 * a, 8 * b, 8), True, False)
                mm(r("pb", a, b), r("N1"), r("OFF", 0, 16 * CS, 16), False, True)

        def greatest(c):
            a, b = CS * c, CS * (c + 1)
            if c < av:
                scan(piece("SAa", c), r("M0"), piece("VA", c), A.min, A.max)
            else:
                scan(piece("SAf", c, 8), r("VF", 16 * a, 16 * b, 2), r("VF", 16 * a + 1, 16 * b, 2), A.max, A.max)
        lead = min(av, CFG["LEAD"]) if t else 1
        for c in range(lead):
            values(CS * c, CS * (c + 1))
        if t and CFG["TUF"] == 1:
            lists()
            wait("first")
        gathered(av)
        if t and CFG["TUF"] == 0:
            lists()
        between = [lambda a=a: values(a, a + CS // 2) for a in range(CS * lead, n0, CS // 2)]
        if t:
            between += [lambda: act(r("OLD"), ind("Y", WY, "TLu", 0, 12), F.Copy),
                        lambda: act(col("CB", 13 + 4 * t), col("CB", 12 + 4 * t), F.Identity, bias=col("CB", 4 * t - 4)),
                        lambda: act(col("CB", 4 * t), col("Q", K), F.Identity, bias=col("CB", 13 + 4 * t), scale=-1.0)]
        for f in between:
            name_a()
            f()
        jp = CFG["JP"][t]
        tail = ((1 if CFG["SGE"] else 0) + (2 if jp == 0 else 0)) if t else 0
        name_a(max(0, na - at["A"] // 12 - tail))
        for c in range(av + 1, K // CS):
            gathered(c)
            if t == 0 and c == K // CS - 1:
                mm(r("pd", 0, NG), r(YW), r("Y", NV, WD), True, False)
                absent(0, 2)
                wanted(2)
                mm(r("m2"), r("PW"), r(W, 1024, NV), True, False)
            least(c - 1)
        if t == 0:
            greatest(av)
        least(K // CS - 1)
        wait("early")
        mm(r("pa", 0, K), r("N1"), r("ZB", 0, K), True, False)
        mm(r("pa", n0, K), r("N1"), r("SBf", 8 * n0, 8 * K, 8), False, False)
        for c in range(av + (t == 0), K // CS):
            greatest(c)
        wait("early2")
        mm(r("pa", n0, K), r("Id"), r("SAf", 8 * n0 + 7, 8 * K, 8), False, False)
        for c in range(av):
            least(c)
            if c == av - 1:
                mm(r("pa", 0, n0), r("N1"), r("SBa", 15, 16 * n0, 16), False, False)
            greatest(c)
        if av:
            mm(r("pa", 0, n0), r("Id"), r("SAa", 15, 16 * n0, 16), False, False)
        ts(r("Qm"), r("pb", 0, K), 0.0, A.is_lt)
        mm(r("pa", 0, K), r("N64"), r("Qm"), False, True)

        def computed(t=t):
            act(r("JK"), r("Qm"), F.Identity, bias=1.0, scale=-1.0, acc=col("CB", 16 + 4 * t))

        def surplus(t=t):
            act(r("EB"), r("ONE"), F.Relu, bias=col("CB", 4 * t), scale=col("CB", 16 + 4 * t))
        if jp == 0:
            computed()
            name_a()
            surplus()
            name_a()
        if t == 0:
            copy(r("PT2"), table(PR0, "RLu"))
            copy(r("CTu"), table(CO0, "RLu"))
            tt(r("Y", *top), r("Y", *top), r("pa", 0, K), A.max)
            mm(r("m2"), r(YW), r("Y", 1024, NV), False, True)
        else:
            mm(r("pd", 0, NG), r(YW), r("Y", NV, WD), True, False)
            wait("new")
            tt(r("NEW"), r("OLD"), r("pa", 0, K), A.max)
            wait("put")
            copy(ind("Y", WY, "TLu", 0, 12), r("NEW"))
            if CFG["SGE"]:
                act(r("SG"), ind("Y", NV, "BDu", 0, 14), F.Sign, bias=0.5)
                name_a()
            if last:
                for (a, b), s in (((0, S0), "s0"), (top, "s1")):
                    dma("S", hbm(T.yy[:, a:b]), r("Y", a, b), s)
            st = (ST * t) % RING
            nb, first = NBR, S0 + st
            wait("ring")
            ts(r("HR", 0, RING - st), r("Y", S0 + st, S0 + RING), 0.0, A.is_ge)
            ts(r("HR", RING - st, RING), r("Y", S0, S0 + st), 0.0, A.is_ge)
            wait("count")
            counted("HR", "RR", nb, 16 * nb)
            for c in range(12):
                a, b = c * nb, (c + 1) * nb
                for u, w in ((a, min(b, 512)), (max(a, 512), b)):
                    if u < w:
                        mm(r("px", u, w), r("N4K"), r("RR", 8 * (u - a) + 7, 8 * (w - a), 8), False, w in (512, 12 * nb), inc=c == 11)
            spread("RR", nb)
            absent(0, 2)
            wait("block")
            scan(back("FS", 0, 12 * nb, 1), back("px", 0, 12 * nb, 1), back(("B1", "MCB")[t - 1], 0, 12 * nb, 1), A.min, A.max, float(first + 16 * nb))
            copy(r("RWR", 0, nb), r("pb", 0, nb))
            wait("place")
            bl = r("FS", 0, 12 * nb, nb)
            ts(r("Bu", 0, 12), bl, -float(first), A.add, 1.0 / 16, A.mult)
            ts(r("BB", 0, 12), bl, S0 + RING - 0.5, A.is_ge, -float(RING), A.mult)
            ts(r("BC", 0, 12), bl, first + RING - 0.5, A.is_ge, float(RING + TOP - st), A.mult)
            tt(r("F2"), ind("RWR", 80, "Bu", 0, 12), r("I16"), A.is_le)
            inside([bl, r("BB", 0, 12)], [r("BC", 0, 12)])
            wait("list")
            copy(r("RLu", 0, 12), r("pc", 0, 12))
            absent(2, 3)
            name_v(K)
            wanted(3)
            copy(r("PT2"), table(PR0, "RLu"))
            copy(r("CTu"), table(CO0, "RLu"))
        dg, hg = CFG["DG"], CFG["HG"][t]
        act(r("OL2"), ind("Y", WY, "RLu", 0, 12), F.Copy)
        for i in range(3):
            act(r("DG", 16 * dg[i], 16 * dg[i + 1]), ind("Y", WY, "PT2", dg[i], dg[i + 1]), F.Relu, scale=-1.0)
            if i == 0 and not (t and CFG["SGE"]):
                act(r("SG"), ind("Y", NV, "BDu", 0, 14), F.Sign, bias=0.5)
        tt(r("NS%d" % t), r("pd", 0, NG), r("Z", NV, WD), A.is_ge)
        send("NS%d" % t, "LN%d" % t, "an%d" % t, "on%d" % t)
        if t == 0:
            const(r("TAB", MO0 + NV - TOP, MO0 + NX), 0)
            const(r("Q", 0, 16), 0)
            for n in ("NH", "NE", "N8"):
                diag(n)
            select(r("BO"), r("ONE", 0, 128), [[-16, 8], [0, 16]], A.is_ge, 0.0, 0)
            select(r("BO"), r("BO"), [[16, 8], [0, 16]], A.is_ge, 0.0, 15, -1)
            iota(r("MCA", 0, (12 - CFG["CA"]) * NBT), [[0, 12 - CFG["CA"]], [128, NBT]], 0)
            const(r("RWT", NBT, 112), 1 << 16)
            const(r("ON5"), 1)
        tt(r(Wn, 0, NV), r("pm"), r("Z", 0, NV), A.is_ge)
        hw = WD + 16

        def consumers(i):
            copy(r("HG", 16 * hg[i], 16 * hg[i + 1]), ind(Wn, hw, "CTu", hg[i], hg[i + 1]))
        act(r("WB"), ind(Wn, NV, "BDu", 0, 14), F.Copy)
        act(r("HG", 16 * hg[4], 16 * K), ind(Wn, hw, "CTu", hg[4], K), F.Copy)
        ksum("pd", "DG", 0, dg[1])
        mm(r("pa", 0, NG), r("NH"), r("SG"), True, False)
        mm(r("pa", 0, NG), r("NE"), r("SG"), False, False)
        mm(r("m0", 0, K), r("N1"), r("ONE"), True, False)
        mm(r("m0", 0, K), r("N1"), r("OL2"), False, False)
        tt(r("OI"), table(MO0, "RLu"), r("OL2"), A.mult)
        consumers(0)
        ksum("pd", "DG", dg[1], dg[2])
        ksum("ph", "HG", 0, hg[1])
        ts(r("OM"), r("OI"), 1, A.bitwise_and)
        consumers(1)
        ksum("pd", "DG", dg[2], K)
        mm(r("pa", 0, NG), r("N1"), r("WB"), False, False)
        facing("LN%d" % t, False)
        ksum("ph", "HG", hg[1], hg[2])
        if jp == 2:
            computed()
        act(r("NF"), r("pa", 0, NG), F.Relu, bias=EPS / 2 - 0.5)
        if jp == 1:
            computed()
        if jp == 2:
            surplus()
        consumers(2)
        tt(r("Ff"), r("OM"), r("pd", 0, K), A.min)
        mm(r("pb", 0, K), r("BO"), r("Ff"), True, True)
        mm(r("m0", 0, K), r("N8"), r("Ff"), False, True)
        if hg[4] > hg[3]:
            consumers(3)
        ksum("ph", "HG", hg[2], K)
        act(r("AB"), r("pb", 0, K), F.Abs, bias=-8.0)
        if jp == 1:
            surplus()
        if CFG["RWV"]:
            act(r("TH"), r("AB"), F.Identity, bias=EPS / 2 - 8.0)
        else:
            mm(r("m1", 0, K), r("N1"), r("AB"), True, False)
        act(r("FR"), r("ph", 0, K), F.Relu, bias=1.0, scale=-1.0)
        tt(ind(Wn, NV, "BDu", 0, 14), r("NF"), r("WB"), A.add)
        if not CFG["RWV"]:
            act(r("TH"), ind(Wn, WY, "RLu", 0, 12), F.Copy, scale=1.0 / EPS)
            mm(r("m1", 0, K), r("Id"), r("TH"), False, True)
        if last:
            act(r("OW", 0, NV), r(Wn, 0, NV), F.Relu, bias=-0.003, scale=1.003)
        if not CFG["RWV"]:
            act(r("RW2"), r("m1", 0, K), F.Sign, bias=8.0)
        scan(r("Q", 1, K + 1), r("FR"), r("EB"), A.add, A.min)
        if CFG["RWV"]:
            tt(r("RW2"), ind(Wn, WY, "RLu", 0, 12), r("TH"), A.is_gt)
        scan(r("GO"), r("Q", 1, K + 1), r("Q", 0, K), A.max, A.subtract)

        def rewant():
            tt(ind(Wn, WY, "RLu", 0, 12), r("GO"), r("RW2"), A.mult)
        if CFG["TO"] == 1 and not last:
            rewant()
        scan(r("TA"), r("GO"), r("m0", 0, K), A.max, A.mult)
        if CFG["TO"] == 2 and not last:
            rewant()
        if CFG["TO"] == 1 and not last:
            counted(Wn, "R", NBT, NV)
        tt(ind("Y", WY, "RLu", 0, 12), r("TA"), r("OL2"), A.add)
        if not last:
            act(r("G%d" % (t + 1)), ind("Y", NV, "BDu", 0, 14), F.Copy)
            send("G%d" % (t + 1), "LG%d" % (t + 1), "ag%d" % (t + 1), "og%d" % (t + 1))
            if t == 0:
                iota(r("BIG", K, RO * K), [[ZMARK[2] - ZMARK[1], 2], [0, K]], ZMARK[1])
                iota(r("T1"), [[16, 12], [0, NBR]], 0)
                for n in ("P4K", "N4K", "Y1"):
                    diag(n)
                iota(r("B1"), [[0, 12], [16, NBR]], S0 + ST % RING)
            else:
                diag("Y2")
                iota(r("MCB"), [[0, 12], [16, NBR]], S0 + 2 * ST % RING)
                const(r("OW", NV, NX), 0)
            const(r("W%d" % (t + 2), NV, WD), 0)
            const(r("W%d" % (t + 2), WD, WY), 1)
            if CFG["TO"] == 0:
                rewant()
            if CFG["TO"] != 1:
                counted(Wn, "R", NBT, NV)
        else:
            ts(r("OY", *ring), r("Y", *ring), -1.0, A.max)
            dma("S", hbm(T.yy[:, ring[0]:ring[1]]), r("OY", *ring), "s4")
            ts(r("OF", *ring), r("Y", *ring), -1.0625, A.is_lt)
            dma("S", hbm(T.yf[:, ring[0]:ring[1]]), r("OF", *ring), "s5")
            tt(ind("OW", NX, "RLu", 0, 12), r("GO"), r("RW2"), A.mult)
            dma("S", hbm(T.yw[:, :]), (T.OW[0:128:16, 0:NV], [("OW", 0, NV)], []), "s6")
    return ops, Q


def emit(g, T, ops, Q):
    total = {}
    for o, nxt in zip(ops, ops[1:]):
        if o["q"] == "P" and nxt["q"] != "P":
            o["inc"] = True
    for o in ops:
        if o["sem"] is None:
            s = "q" + o["q"]
            total[s] = total.get(s, 0) + (1 if o["inc"] else 0)
            o["s"], o["n"] = s, total[s] + (0 if o["inc"] else 1)
        else:
            total[o["sem"]] = total.get(o["sem"], 0) + o["cnt"]
    seen = {}
    known = {q: {} for q in Q}
    hist = {}
    for o in ops:
        q = o["q"]
        if o["sem"] is not None:
            o["s"], o["n"] = o["sem"], total[o["sem"]]
        need = {}
        for acc, w in [(x, False) for x in o["rd"]] + [(x, True) for x in o["wr"]]:
            bank = acc[0] in BANKS
            for a, b, pw, p in hist.get(acc[0], []):
                if p is o:
                    continue
                if bank and p["q"] != q:
                    hit = True
                else:
                    hit = (w or pw) and a < acc[2] and acc[1] < b
                    if hit and p["q"] == q == "P":
                        hit = False
                    if hit and p["sem"] is not None and p["sem"] == o["sem"]:
                        hit = False
                if hit and need.get(p["s"], (0, None))[0] < p["n"]:
                    need[p["s"]] = (p["n"], p)
        if q != "X":
            kn = known[q]
            for s in sorted(need, key=lambda s: -need[s][1]["i"]):
                n, p = need[s]
                if kn.get(s, 0) < n:
                    Q[q].wait_ge(T.sem[s], n)
                    seen[s] = max(seen.get(s, 0), n)
                    kn[s] = n
                    for s2, n2 in p["k"].items():
                        kn[s2] = max(kn.get(s2, 0), n2)
            ins = o["fn"]()
            if ins is not None and o["inc"]:
                ins.then_inc(T.sem[o["s"]], 1 if o["sem"] is None else 16)
            o["k"] = dict(kn) if o["sem"] is None else {}
        else:
            o["k"] = {}
        o["i"] = len(hist.setdefault("", []))
        hist[""].append(0)
        for acc in o["rd"]:
            hist.setdefault(acc[0], []).append((acc[1], acc[2], False, o))
        for acc in o["wr"]:
            hist.setdefault(acc[0], []).append((acc[1], acc[2], True, o))
    for s in total:
        if seen.get(s, 0) < total[s]:
            g.wait_ge(T.sem[s], total[s])


def rank_program(g, core, T, topo):
    if T.rank_of(core) is None:
        return
    ops, Q = build(g, core, T, topo)
    emit(g, T, ops, Q)
